import numpy as np
import ml_dtypes


def mxq(x, axis, fmt="e4m3"):
    dtype, down = {"e4m3": (ml_dtypes.float8_e4m3fn, 7), "e5m2": (ml_dtypes.float8_e5m2, 14)}[fmt]
    v = np.moveaxis(np.asarray(x, np.float32).astype(ml_dtypes.bfloat16).astype(np.float64), axis, -1)
    blocks = v.reshape(v.shape[:-1] + (-1, 32))
    amax = np.abs(blocks).max(-1, keepdims=True)
    byte = np.maximum(np.where(amax > 0, np.frexp(amax)[1] - 1 + 127, 0) - down, 1)
    scale = np.exp2(byte - 127.0)
    codes = (blocks / scale).astype(np.float32).astype(dtype).astype(np.float64)
    return np.moveaxis((codes * scale).reshape(v.shape), -1, axis)


WIDE = False


def mx_kscale(k):
    if not WIDE:
        return np.ones(k)
    levels = np.array([10, -10, 5, -5, 0])
    if k % 512:
        return np.exp2(np.random.permutation(np.resize(levels, k // 32))).repeat(32)
    a = np.empty((k // 512, 16))
    for p in range(k // 512):
        a[p, :8] = np.random.permutation(np.resize(levels, 8))
        for g in range(8):
            far = levels[np.abs(levels - a[p, g]) >= 10]
            a[p, g + 8] = far[np.random.randint(len(far))]
    return np.exp2(a.ravel()).repeat(32)


def f64(x):
    return np.asarray(x).astype(np.float64)


def striped(idx):
    return np.tile(idx.reshape(-1, 16).T, (8, 1)).astype(np.uint16)


def unstriped(offs):
    return offs[:16].T.reshape(-1).astype(np.int64)


E2M1 = np.array([0.0, 0.5, 1.0, 1.5, 2.0, 3.0, 4.0, 6.0, -0.0, -0.5, -1.0, -1.5, -2.0, -3.0, -4.0, -6.0])


def pack_fp4(w):
    k, n = w.shape
    w = f64(np.asarray(w, np.float32).astype(ml_dtypes.bfloat16)).reshape(k // 32, 32, n)
    amax = np.abs(w).max(1)
    mant, ex = np.frexp(amax / 6.0)
    byte = np.clip(np.where(amax > 0, np.where(mant > 0.5, ex, ex - 1) + 127, 1), 1, 254)
    scaled = (w * np.exp2(127.0 - byte)[:, None, :]).reshape(k, n).astype(np.float32)
    c = np.ascontiguousarray(scaled.reshape(k // 512, 128, 4, n).transpose(0, 1, 3, 2)).astype(ml_dtypes.float4_e2m1fn).view(np.uint8) & 0xF
    words = (c[..., 0::2] | (c[..., 1::2] << 4)).reshape(k // 512, 128, 2 * n)
    return np.ascontiguousarray(words), np.ascontiguousarray(byte.astype(np.uint8).reshape(k // 512, 16, n))


def unpack_fp4(words, scales):
    g, _, n = scales.shape
    words = np.ascontiguousarray(words).reshape(g, 128, n, 2)
    nib = np.empty((g, 128, n, 4), np.uint8)
    nib[..., 0::2] = words & 0xF
    nib[..., 1::2] = words >> 4
    vals = E2M1[nib] * np.repeat(np.exp2(scales.astype(np.float64) - 127.0), 8, axis=1)[..., None]
    return vals.transpose(0, 1, 3, 2).reshape(g * 512, n)


K, T, H, N = 512, 512, 512, 256


def setup_inputs():
    n = np.random.standard_normal
    s = mx_kscale(K)[:, None]
    u = mx_kscale(H)
    packed_xT = pack_fp4(n((K, T)) * s)
    return {
        "x_words": packed_xT[0],
        "x_scales": packed_xT[1],
        "w1": (n((K, H)) / np.sqrt(K) / s * u).astype(np.float32),
        "w2": (n((H, N)) / np.sqrt(3 * H) / u[:, None]).astype(np.float32),
        "w3": (n((H, N)) / np.sqrt(3 * H) / u[:, None]).astype(np.float32),
        "w4": (n((H, N)) / np.sqrt(3 * H) / u[:, None]).astype(np.float32),
        "pos1": striped(np.random.permutation(T)),
        "pos2": striped(np.random.permutation(T)),
        "pos3": striped(np.random.permutation(T)),
    }


def reference(x_words, x_scales, w1, w2, w3, w4, pos1, pos2, pos3):
    xq = unpack_fp4(x_words, x_scales)
    h = mxq(f64(w1), 0, "e4m3").T @ xq
    g0 = h[:, unstriped(pos1)]
    g1 = h[:, unstriped(pos2)]
    g2 = h[:, unstriped(pos3)]
    z1 = (g0 + g1 + g2) / 3
    z2 = np.maximum(np.maximum(g0, g1), g2)
    z3 = np.minimum(np.minimum(g0, g1), g2)
    return mxq(f64(w2), 0, "e4m3").T @ mxq(z1, 0, "e4m3") + mxq(f64(w3), 0, "e4m3").T @ mxq(z2, 0, "e4m3") + mxq(f64(w4), 0, "e4m3").T @ mxq(z3, 0, "e4m3")

@@ -1,0 +1,211 @@
+from contextlib import ExitStack
+
+import concourse.mybir as mybir
+from concourse.masks import make_identity
+
+K, T, H, N = 512, 512, 512, 256
+FLOPS = 2 * K * H * T + 3 * 2 * H * N * T
+
+F32 = mybir.dt.float32
+BF16 = mybir.dt.bfloat16
+I32 = mybir.dt.int32
+U32 = mybir.dt.uint32
+U16 = mybir.dt.uint16
+U8 = mybir.dt.uint8
+FP8X4 = mybir.dt.float8_e4m3fn_x4
+FP4X4 = mybir.dt.float4_e2m1fn_x4
+COPY = mybir.ActivationFunctionType.Copy
+MAX = mybir.AluOpType.max
+MIN = mybir.AluOpType.min
+
+P = 128
+PACK = 4
+WINDOW = 704
+LINE = 4
+W1_SPLIT = 384
+HALF = T // 2
+
+
+def tile_picked_wpna_none_l_kernel(
+    tc, x_words, x_scales, w1, w2, w3, w4, pos1, pos2, pos3, out
+):
+    nc = tc.nc
+    with ExitStack() as ctx:
+        sb = ctx.enter_context(tc.tile_pool(name="sb", bufs=1))
+        ps = ctx.enter_context(tc.psum_pool(name="ps", bufs=1))
+
+        def bank(b, shape, name):
+            return ps.tile(shape, F32, name=name, tag="bank%d" % b)
+
+        w1_rows = w1.rearrange("(p j) c -> p j c", j=PACK)
+        w1_parts = [(0, W1_SPLIT), (W1_SPLIT, H)]
+        w1_raw = []
+        for a, b in w1_parts:
+            raw = sb.tile([P, PACK, b - a], F32, name="w1_raw%d" % a)
+            nc.sync.dma_start(out=raw[:], in_=w1_rows[:, :, a:b])
+            w1_raw.append(raw)
+        xw = sb.tile([P, 2 * T], U8, name="xw", align_bytes=64)
+        nc.sync.dma_start(out=xw[:].bitcast(I32), in_=x_words[0].bitcast(I32))
+        xs = sb.tile([P, T], U8, name="xs", align_bytes=64)
+        nc.vector.memset(xs[:].bitcast(I32), 0)
+        for q in range(4):
+            nc.scalar.dma_start(
+                out=xs[32 * q : 32 * q + 4, :].bitcast(I32), in_=x_scales[0, 4 * q : 4 * q + 4, :].bitcast(I32)
+            )
+        lists = [sb.tile([P, T // 16], U16, name="pos%d" % d) for d in range(3)]
+        nc.sync.dma_start(lists[0][:], pos1)
+        wz_raw = []
+        for s, w in enumerate((w2, w3, w4)):
+            raw = sb.tile([P, PACK, N], F32, name="wz_raw%d" % s)
+            nc.sync.dma_start(out=raw[:], in_=w.rearrange("(p j) c -> p j c", j=PACK))
+            wz_raw.append(raw)
+        nc.sync.dma_start(lists[1][:], pos2)
+        nc.sync.dma_start(lists[2][:], pos3)
+
+        ident = sb.tile([P, P], F32, name="ident")
+        make_identity(nc, ident[:])
+
+        zeros = sb.tile([P, WINDOW - T], F32, name="zeros")
+        nc.vector.memset(zeros[:], 0.0)
+        h = [sb.tile([P, WINDOW], F32, name="h%d" % t) for t in range(PACK)]
+        for t in range(PACK):
+            nc.scalar.activation(h[t][:, T:], zeros[:], COPY)
+
+        w1_grp = sb.tile([P, PACK, P, PACK], BF16, name="w1_grp", align_bytes=64)
+        for (a, b), raw in zip(w1_parts, w1_raw):
+            nc.vector.tensor_copy(
+                out=w1_grp[:, :, a // PACK : b // PACK, :].rearrange("p t m j -> p m j t"),
+                in_=raw[:].rearrange("p j (m t) -> p m j t", t=PACK),
+            )
+        w1_codes = sb.tile([P, PACK, P], U32, name="w1_codes", align_bytes=64)
+        w1_scales = sb.tile([P, PACK, P], U8, name="w1_scales", align_bytes=64)
+        for t in range(PACK):
+            nc.vector.quantize_mx(
+                out=w1_codes[:, t, :].bitcast(FP8X4),
+                scales=w1_scales[:, t, :],
+                in_=w1_grp[:, t, :, :].rearrange("p m j -> p (m j)"),
+            )
+            pieces = [(0, HALF), (HALF, T)] if t == 0 else [(0, T)]
+            for a, b in pieces:
+                acc = bank((t + 1) % 4 if b == T else 0, [P, b - a], "h_acc%d_%d" % (t, a))
+                nc.tensor.matmul_mx(
+                    out=acc[:],
+                    lhsT=w1_codes[:, t, :].bitcast(FP8X4),
+                    lhsT_scale=w1_scales[:, t, :],
+                    rhs=xw[:, 2 * a : 2 * b].bitcast(FP4X4),
+                    rhs_scale=xs[:, a:b],
+                    start=True,
+                    stop=True,
+                )
+                if a == HALF:
+                    nc.vector.tensor_copy(out=h[t][:, a:b], in_=acc[:])
+                else:
+                    nc.scalar.copy(out=h[t][:, a:b], in_=acc[:])
+
+        def interleave(dst, src):
+            nc.scalar.copy(
+                out=dst.rearrange("p (c i) t -> p c t i", i=LINE),
+                in_=src.rearrange("p t (c i) -> p c t i", i=LINE),
+            )
+
+        wz_grp = []
+        for s in range(3):
+            grp = sb.tile([P, N, PACK], BF16, name="wz_grp%d" % s, align_bytes=64)
+            interleave(grp[:], wz_raw[s][:])
+            wz_grp.append(grp)
+
+        sums = [bank(4 + b, [P, PACK, P], "sum%d" % b) for b in range(T // P)]
+
+        def gather(d, v0, v1):
+            g = sb.tile([P, PACK, v1 - v0], F32, name="g%d_%d" % (d, v0))
+            for t in range(PACK):
+                nc.vector.tensor_copy(g[:, t, :], h[t][:].indirect(lists[d][:, v0 // 16 : v1 // 16]))
+                for b in range(v0 // P, v1 // P):
+                    nc.tensor.matmul(
+                        sums[b][:, t, :],
+                        lhsT=g[:, t, b * P - v0 : (b + 1) * P - v0],
+                        rhs=ident[:],
+                        is_transpose=True,
+                        start=(d == 0 and t == 0),
+                        stop=(d == 2 and t == PACK - 1),
+                    )
+            gb = sb.tile([P, v1 - v0, PACK], BF16, name="gb%d_%d" % (d, v0), align_bytes=64)
+            interleave(gb[:], g[:])
+            return gb
+
+        gb0 = gather(0, 0, T)
+        gb1 = gather(1, 0, T)
+        gb2 = []
+        z_mean = []
+        for c in range(2):
+            v0 = c * HALF
+            gb2.append(gather(2, v0, v0 + HALF))
+            words = bank(c, [P, 2, 2, P], "words%d" % c)
+            for bb in range(2):
+                mean_t = sb.tile([P, 2, P, 2], BF16, name="mean_t%d_%d" % (c, bb))
+                nc.scalar.activation(
+                    mean_t[:],
+                    sums[2 * c + bb][:].rearrange("v (u e) p -> v u p e", e=2),
+                    COPY,
+                    scale=1.0 / 3.0,
+                )
+                pairs = mean_t[:].rearrange("v u p e -> v (u p e)").bitcast(F32)
+                for u in range(2):
+                    nc.tensor.transpose(words[:, bb, u, :], pairs[:, u * P : (u + 1) * P], ident[:])
+            zm = sb.tile([P, HALF * PACK], BF16, name="z_mean%d" % c, align_bytes=64)
+            nc.scalar.copy(
+                out=zm[:].bitcast(F32).rearrange("p (b v u) -> p b v u", b=2, u=2),
+                in_=words[:].rearrange("p b u v -> p b v u"),
+            )
+            z_mean.append(zm)
+
+        wz_codes = sb.tile([P, 3, N], U32, name="wz_codes", align_bytes=64)
+        wz_scales = sb.tile([P, 3, N], U8, name="wz_scales", align_bytes=64)
+        for s in range(3):
+            nc.vector.quantize_mx(
+                out=wz_codes[:, s, :].bitcast(FP8X4),
+                scales=wz_scales[:, s, :],
+                in_=wz_grp[s][:].rearrange("p c j -> p (c j)"),
+            )
+
+        hi01 = sb.tile([P, T * PACK], BF16, name="hi01")
+        lo01 = sb.tile([P, T * PACK], BF16, name="lo01")
+        flat0 = gb0[:].rearrange("p v t -> p (v t)")
+        flat1 = gb1[:].rearrange("p v t -> p (v t)")
+        nc.vector.tensor_tensor(hi01[:], flat0, flat1, MAX)
+        nc.vector.tensor_tensor(lo01[:], flat0, flat1, MIN)
+
+        out_rows = out.rearrange("(mt p) v -> p mt v", p=P)
+        for c in range(2):
+            cols = slice(c * HALF * PACK, (c + 1) * HALF * PACK)
+            flat2 = gb2[c][:].rearrange("p v t -> p (v t)")
+            z_max = sb.tile([P, HALF * PACK], BF16, name="z_max%d" % c, align_bytes=64)
+            z_min = sb.tile([P, HALF * PACK], BF16, name="z_min%d" % c, align_bytes=64)
+            nc.vector.tensor_tensor(z_max[:], hi01[:, cols], flat2, MAX)
+            nc.vector.tensor_tensor(z_min[:], lo01[:, cols], flat2, MIN)
+            passes = []
+            for s, z in ((0, z_mean[c]), (1, z_max), (2, z_min)):
+                codes = sb.tile([P, HALF], U32, name="z_codes%d_%d" % (c, s), align_bytes=64)
+                scales = sb.tile([P, HALF], U8, name="z_scales%d_%d" % (c, s), align_bytes=64)
+                nc.vector.quantize_mx(out=codes[:].bitcast(FP8X4), scales=scales[:], in_=z[:])
+                passes.append((s, codes[:], scales[:]))
+            accs = [bank((2 + 2 * c + mt) % 8, [P, HALF], "o_acc%d_%d" % (c, mt)) for mt in range(2)]
+            for n_pass, (s, codes, scales) in enumerate(passes):
+                for mt in range(2):
+                    nc.tensor.matmul_mx(
+                        out=accs[mt][:],
+                        lhsT=wz_codes[:, s, mt * P : (mt + 1) * P].bitcast(FP8X4),
+                        lhsT_scale=wz_scales[:, s, mt * P : (mt + 1) * P],
+                        rhs=codes.bitcast(FP8X4),
+                        rhs_scale=scales,
+                        start=(n_pass == 0),
+                        stop=(n_pass == 2),
+                    )
+            for mt in range(2):
+                res = sb.tile([P, HALF], F32, name="res%d_%d" % (c, mt))
+                if c == 1 and mt == 1:
+                    nc.vector.tensor_copy(out=res[:], in_=accs[mt][:])
+                    nc.scalar.dma_start(out=out_rows[:, mt, c * HALF : (c + 1) * HALF], in_=res[:])
+                else:
+                    nc.scalar.copy(out=res[:], in_=accs[mt][:])
+                    nc.sync.dma_start(out=out_rows[:, mt, c * HALF : (c + 1) * HALF], in_=res[:])

@@ -22,7 +22,9 @@ P = 128
 PACK = 4
 WINDOW = 704
 LINE = 4
-W1_SPLIT = 384
+FIRST_V = 96
+REST_FILL = 40
+REST_V = 76
 HALF = T // 2
 
 
@@ -32,24 +34,20 @@ def tile_picked_wpna_none_l_kernel(
     nc = tc.nc
     with ExitStack() as ctx:
         sb = ctx.enter_context(tc.tile_pool(name="sb", bufs=1))
+        late = ctx.enter_context(tc.tile_pool(name="late", bufs=1))
         ps = ctx.enter_context(tc.psum_pool(name="ps", bufs=1))
 
         def bank(b, shape, name):
             return ps.tile(shape, F32, name=name, tag="bank%d" % b)
 
-        w1_rows = w1.rearrange("(p j) c -> p j c", j=PACK)
-        w1_parts = [(0, W1_SPLIT), (W1_SPLIT, H)]
-        w1_raw = []
-        for a, b in w1_parts:
-            raw = sb.tile([P, PACK, b - a], F32, name="w1_raw%d" % a)
-            nc.sync.dma_start(out=raw[:], in_=w1_rows[:, :, a:b])
-            w1_raw.append(raw)
+        w1_raw = sb.tile([P, PACK, H], F32, name="w1_raw")
+        nc.sync.dma_start(out=w1_raw[:], in_=w1.rearrange("(p j) c -> p j c", j=PACK))
         xw = sb.tile([P, 2 * T], U8, name="xw", align_bytes=64)
         nc.sync.dma_start(out=xw[:].bitcast(I32), in_=x_words[0].bitcast(I32))
         xs = sb.tile([P, T], U8, name="xs", align_bytes=64)
         nc.vector.memset(xs[:].bitcast(I32), 0)
         for q in range(4):
-            nc.scalar.dma_start(
+            nc.sync.dma_start(
                 out=xs[32 * q : 32 * q + 4, :].bitcast(I32), in_=x_scales[0, 4 * q : 4 * q + 4, :].bitcast(I32)
             )
         lists = [sb.tile([P, T // 16], U16, name="pos%d" % d) for d in range(3)]
@@ -59,31 +57,40 @@ def tile_picked_wpna_none_l_kernel(
             raw = sb.tile([P, PACK, N], F32, name="wz_raw%d" % s)
             nc.sync.dma_start(out=raw[:], in_=w.rearrange("(p j) c -> p j c", j=PACK))
             wz_raw.append(raw)
-        nc.sync.dma_start(lists[1][:], pos2)
-        nc.sync.dma_start(lists[2][:], pos3)
+            if s == 0:
+                nc.sync.dma_start(lists[1][:], pos2)
+                nc.sync.dma_start(lists[2][:], pos3)
 
         ident = sb.tile([P, P], F32, name="ident")
         make_identity(nc, ident[:])
 
         zeros = sb.tile([P, WINDOW - T], F32, name="zeros")
         nc.vector.memset(zeros[:], 0.0)
+        plane_bytes = 4 * PACK * T
+        unit = late.tile([P, PACK * HALF + 16], F32, name="unit", offset=plane_bytes - 32)
+        nc.vector.memset(unit[:, 0:1], 1.0)
         h = [sb.tile([P, WINDOW], F32, name="h%d" % t) for t in range(PACK)]
         for t in range(PACK):
             nc.scalar.activation(h[t][:, T:], zeros[:], COPY)
 
-        w1_grp = sb.tile([P, PACK, P, PACK], BF16, name="w1_grp", align_bytes=64)
-        for (a, b), raw in zip(w1_parts, w1_raw):
-            nc.vector.tensor_copy(
-                out=w1_grp[:, :, a // PACK : b // PACK, :].rearrange("p t m j -> p m j t"),
-                in_=raw[:].rearrange("p j (m t) -> p m j t", t=PACK),
-            )
+        w1_first = sb.tile([P, P, PACK], BF16, name="w1_first", align_bytes=64)
+        w1_rest = sb.tile([P, PACK - 1, P, PACK], BF16, name="w1_rest", align_bytes=64)
+        w1_view = w1_raw[:].rearrange("p j (m t) -> p m j t", t=PACK)
+        rest_view = w1_rest[:].rearrange("p t m j -> p m j t")
+        nc.vector.tensor_copy(out=w1_first[:, :FIRST_V, :], in_=w1_view[:, :FIRST_V, :, 0])
+        nc.scalar.copy(out=w1_first[:, FIRST_V:, :], in_=w1_view[:, FIRST_V:, :, 0])
+        nc.scalar.copy(out=rest_view[:, REST_V:], in_=w1_view[:, REST_V:, :, 1:])
+        w1_grp = [w1_first[:]] + [w1_rest[:, t, :, :] for t in range(PACK - 1)]
         w1_codes = sb.tile([P, PACK, P], U32, name="w1_codes", align_bytes=64)
         w1_scales = sb.tile([P, PACK, P], U8, name="w1_scales", align_bytes=64)
         for t in range(PACK):
+            if t == 1:
+                for a, b in ((0, REST_FILL), (REST_FILL, REST_V)):
+                    nc.vector.tensor_copy(out=rest_view[:, a:b], in_=w1_view[:, a:b, :, 1:])
             nc.vector.quantize_mx(
                 out=w1_codes[:, t, :].bitcast(FP8X4),
                 scales=w1_scales[:, t, :],
-                in_=w1_grp[:, t, :, :].rearrange("p m j -> p (m j)"),
+                in_=w1_grp[t].rearrange("p m j -> p (m j)"),
             )
             pieces = [(0, HALF), (HALF, T)] if t == 0 else [(0, T)]
             for a, b in pieces:
@@ -99,6 +106,8 @@ def tile_picked_wpna_none_l_kernel(
                 )
                 if a == HALF:
                     nc.vector.tensor_copy(out=h[t][:, a:b], in_=acc[:])
+                elif t == PACK - 1:
+                    nc.scalar.activation(h[t][:, a:b], acc[:], COPY, scale=unit[:, 0:1])
                 else:
                     nc.scalar.copy(out=h[t][:, a:b], in_=acc[:])
 
@@ -117,7 +126,12 @@ def tile_picked_wpna_none_l_kernel(
         sums = [bank(4 + b, [P, PACK, P], "sum%d" % b) for b in range(T // P)]
 
         def gather(d, v0, v1):
-            g = sb.tile([P, PACK, v1 - v0], F32, name="g%d_%d" % (d, v0))
+            if d == 0:
+                g = sb.tile([P, PACK, v1 - v0], F32, name="g0")
+            else:
+                g = late.tile(
+                    [P, PACK, v1 - v0], F32, name="g%d_%d" % (d, v0), offset=(d - 1) * plane_bytes + 4 * PACK * v0
+                )
             for t in range(PACK):
                 nc.vector.tensor_copy(g[:, t, :], h[t][:].indirect(lists[d][:, v0 // 16 : v1 // 16]))
                 for b in range(v0 // P, v1 // P):
@@ -142,7 +156,7 @@ def tile_picked_wpna_none_l_kernel(
             gb2.append(gather(2, v0, v0 + HALF))
             words = bank(c, [P, 2, 2, P], "words%d" % c)
             for bb in range(2):
-                mean_t = sb.tile([P, 2, P, 2], BF16, name="mean_t%d_%d" % (c, bb))
+                mean_t = sb.tile([P, 2, P, 2], BF16, name="mean_t%d_%d" % (c, bb), tag="stage%d_%d" % (c, bb))
                 nc.scalar.activation(
                     mean_t[:],
                     sums[2 * c + bb][:].rearrange("v (u e) p -> v u p e", e=2),
@@ -183,29 +197,54 @@ def tile_picked_wpna_none_l_kernel(
             z_min = sb.tile([P, HALF * PACK], BF16, name="z_min%d" % c, align_bytes=64)
             nc.vector.tensor_tensor(z_max[:], hi01[:, cols], flat2, MAX)
             nc.vector.tensor_tensor(z_min[:], lo01[:, cols], flat2, MIN)
-            passes = []
-            for s, z in ((0, z_mean[c]), (1, z_max), (2, z_min)):
+            quantised = {}
+            for s, z in ((1, z_max), (2, z_min), (0, z_mean[c])):
                 codes = sb.tile([P, HALF], U32, name="z_codes%d_%d" % (c, s), align_bytes=64)
                 scales = sb.tile([P, HALF], U8, name="z_scales%d_%d" % (c, s), align_bytes=64)
-                nc.vector.quantize_mx(out=codes[:].bitcast(FP8X4), scales=scales[:], in_=z[:])
-                passes.append((s, codes[:], scales[:]))
-            accs = [bank((2 + 2 * c + mt) % 8, [P, HALF], "o_acc%d_%d" % (c, mt)) for mt in range(2)]
-            for n_pass, (s, codes, scales) in enumerate(passes):
+                quantised[s] = (z, codes, scales)
+
+            def quantise(s, a, b):
+                z, codes, scales = quantised[s]
+                nc.vector.quantize_mx(
+                    out=codes[:, a:b].bitcast(FP8X4), scales=scales[:, a:b], in_=z[:, a * PACK : b * PACK]
+                )
+
+            def product(acc, s, mt, a, b):
+                z, codes, scales = quantised[s]
+                nc.tensor.matmul_mx(
+                    out=acc[:],
+                    lhsT=wz_codes[:, s, mt * P : (mt + 1) * P].bitcast(FP8X4),
+                    lhsT_scale=wz_scales[:, s, mt * P : (mt + 1) * P],
+                    rhs=codes[:, a:b].bitcast(FP8X4),
+                    rhs_scale=scales[:, a:b],
+                    start=(s == 1),
+                    stop=(s == 0),
+                )
+
+            pieces = [(0, HALF)] if c == 0 else [(0, P), (P, HALF)]
+            accs = {}
+            for n_piece, (a, b) in enumerate(pieces):
                 for mt in range(2):
-                    nc.tensor.matmul_mx(
-                        out=accs[mt][:],
-                        lhsT=wz_codes[:, s, mt * P : (mt + 1) * P].bitcast(FP8X4),
-                        lhsT_scale=wz_scales[:, s, mt * P : (mt + 1) * P],
-                        rhs=codes.bitcast(FP8X4),
-                        rhs_scale=scales,
-                        start=(n_pass == 0),
-                        stop=(n_pass == 2),
-                    )
-            for mt in range(2):
-                res = sb.tile([P, HALF], F32, name="res%d_%d" % (c, mt))
-                if c == 1 and mt == 1:
-                    nc.vector.tensor_copy(out=res[:], in_=accs[mt][:])
-                    nc.scalar.dma_start(out=out_rows[:, mt, c * HALF : (c + 1) * HALF], in_=res[:])
+                    accs[a, mt] = bank(2 + 2 * (c + n_piece) + mt, [P, b - a], "o_acc%d_%d_%d" % (c, a, mt))
+            for s in (1, 2):
+                quantise(s, 0, HALF)
+                for a, b in pieces:
+                    for mt in range(2):
+                        product(accs[a, mt], s, mt, a, b)
+            for a, b in pieces:
+                quantise(0, a, b)
+                for mt in range(2):
+                    product(accs[a, mt], 0, mt, a, b)
+                if c == 0:
+                    for mt in range(2):
+                        res = sb.tile([P, HALF], F32, name="res_first%d" % mt, tag="stage1_%d" % mt)
+                        nc.scalar.copy(out=res[:], in_=accs[a, mt][:])
+                        nc.sync.dma_start(out=out_rows[:, mt, :HALF], in_=res[:])
                 else:
-                    nc.scalar.copy(out=res[:], in_=accs[mt][:])
-                    nc.sync.dma_start(out=out_rows[:, mt, c * HALF : (c + 1) * HALF], in_=res[:])
+                    res = sb.tile([P, 2, P], F32, name="res_last%d" % a)
+                    nc.scalar.copy(out=res[:, 0, :], in_=accs[a, 0][:])
+                    if a == 0:
+                        nc.scalar.copy(out=res[:, 1, :], in_=accs[a, 1][:])
+                    else:
+                        nc.vector.tensor_copy(out=res[:, 1, :], in_=accs[a, 1][:])
+                    nc.sync.dma_start(out=out_rows[:, :, HALF + a : HALF + b], in_=res[:])

@@ -92,9 +92,9 @@ def tile_picked_wpna_none_l_kernel(
                 scales=w1_scales[:, t, :],
                 in_=w1_grp[t].rearrange("p m j -> p (m j)"),
             )
-            pieces = [(0, HALF), (HALF, T)] if t == 0 else [(0, T)]
-            for a, b in pieces:
-                acc = bank((t + 1) % 4 if b == T else 0, [P, b - a], "h_acc%d_%d" % (t, a))
+            pieces = [(0, P, 7), (P, T - P, 0), (T - P, T, 1)] if t == 0 else [(0, T, (t + 1) % 4)]
+            for a, b, n_bank in pieces:
+                acc = bank(n_bank, [P, b - a], "h_acc%d_%d" % (t, a))
                 nc.tensor.matmul_mx(
                     out=acc[:],
                     lhsT=w1_codes[:, t, :].bitcast(FP8X4),
@@ -104,7 +104,7 @@ def tile_picked_wpna_none_l_kernel(
                     start=True,
                     stop=True,
                 )
-                if a == HALF:
+                if b == P:
                     nc.vector.tensor_copy(out=h[t][:, a:b], in_=acc[:])
                 elif t == PACK - 1:
                     nc.scalar.activation(h[t][:, a:b], acc[:], COPY, scale=unit[:, 0:1])
@@ -143,7 +143,8 @@ def tile_picked_wpna_none_l_kernel(
                         start=(d == 0 and t == 0),
                         stop=(d == 2 and t == PACK - 1),
                     )
-            gb = sb.tile([P, v1 - v0, PACK], BF16, name="gb%d_%d" % (d, v0), align_bytes=64)
+            gb = sb.tile([P, v1 - v0, PACK], BF16, name="gb%d_%d" % (d, v0), align_bytes=64,
+                tag="stage0_1" if v0 == HALF else "gb%d" % d)
             interleave(gb[:], g[:])
             return gb
 
@@ -156,7 +157,7 @@ def tile_picked_wpna_none_l_kernel(
             gb2.append(gather(2, v0, v0 + HALF))
             words = bank(c, [P, 2, 2, P], "words%d" % c)
             for bb in range(2):
-                mean_t = sb.tile([P, 2, P, 2], BF16, name="mean_t%d_%d" % (c, bb), tag="stage%d_%d" % (c, bb))
+                mean_t = sb.tile([P, 2, P, 2], BF16, name="mean_t%d_%d" % (c, bb), tag="stage%d_%d" % (c, bb), align_bytes=64)
                 nc.scalar.activation(
                     mean_t[:],
                     sums[2 * c + bb][:].rearrange("v (u e) p -> v u p e", e=2),
@@ -237,7 +238,7 @@ def tile_picked_wpna_none_l_kernel(
                     product(accs[a, mt], 0, mt, a, b)
                 if c == 0:
                     for mt in range(2):
-                        res = sb.tile([P, HALF], F32, name="res_first%d" % mt, tag="stage1_%d" % mt)
+                        res = sb.tile([P, HALF], F32, name="res_first%d" % mt, tag="stage1_%d" % mt, align_bytes=64)
                         nc.scalar.copy(out=res[:], in_=accs[a, mt][:])
                         nc.sync.dma_start(out=out_rows[:, mt, :HALF], in_=res[:])
                 else:

@@ -22,9 +22,7 @@ P = 128
 PACK = 4
 WINDOW = 704
 LINE = 4
-FIRST_V = 96
-REST_FILL = 40
-REST_V = 76
+RUN = 8
 HALF = T // 2
 
 
@@ -55,11 +53,13 @@ def tile_picked_wpna_none_l_kernel(
         wz_raw = []
         for s, w in enumerate((w2, w3, w4)):
             raw = sb.tile([P, PACK, N], F32, name="wz_raw%d" % s)
-            nc.sync.dma_start(out=raw[:], in_=w.rearrange("(p j) c -> p j c", j=PACK))
-            wz_raw.append(raw)
             if s == 0:
                 nc.sync.dma_start(lists[1][:], pos2)
                 nc.sync.dma_start(lists[2][:], pos3)
+            rows = w.rearrange("(g u r e) c -> u g r (e c)", u=2, r=RUN, e=2)
+            for u in range(2):
+                nc.sync.dma_start(out=raw[:, 2 * u : 2 * u + 2, :].rearrange("p e c -> p (e c)"), in_=rows[u])
+            wz_raw.append(raw)
 
         ident = sb.tile([P, P], F32, name="ident")
         make_identity(nc, ident[:])
@@ -73,26 +73,34 @@ def tile_picked_wpna_none_l_kernel(
         for t in range(PACK):
             nc.scalar.activation(h[t][:, T:], zeros[:], COPY)
 
-        w1_first = sb.tile([P, P, PACK], BF16, name="w1_first", align_bytes=64)
-        w1_rest = sb.tile([P, PACK - 1, P, PACK], BF16, name="w1_rest", align_bytes=64)
-        w1_view = w1_raw[:].rearrange("p j (m t) -> p m j t", t=PACK)
-        rest_view = w1_rest[:].rearrange("p t m j -> p m j t")
-        nc.vector.tensor_copy(out=w1_first[:, :FIRST_V, :], in_=w1_view[:, :FIRST_V, :, 0])
-        nc.scalar.copy(out=w1_first[:, FIRST_V:, :], in_=w1_view[:, FIRST_V:, :, 0])
-        nc.scalar.copy(out=rest_view[:, REST_V:], in_=w1_view[:, REST_V:, :, 1:])
-        w1_grp = [w1_first[:]] + [w1_rest[:, t, :, :] for t in range(PACK - 1)]
+        w1_grp = sb.tile([P, PACK, P, PACK], BF16, name="w1_grp", align_bytes=64)
+        w1_from = w1_raw[:].rearrange("p j (g u a i e) -> p u e g a j i", u=2, a=RUN // LINE, i=LINE, e=2)
+        w1_into = w1_grp[:].rearrange("p t (g a i) j -> p t g a j i", a=RUN // LINE, i=LINE)
         w1_codes = sb.tile([P, PACK, P], U32, name="w1_codes", align_bytes=64)
         w1_scales = sb.tile([P, PACK, P], U8, name="w1_scales", align_bytes=64)
-        for t in range(PACK):
-            if t == 1:
-                for a, b in ((0, REST_FILL), (REST_FILL, REST_V)):
-                    nc.vector.tensor_copy(out=rest_view[:, a:b], in_=w1_view[:, a:b, :, 1:])
+
+        def w1_round(copy, t, g0, g1):
+            copy(out=w1_into[:, t, g0:g1], in_=w1_from[:, t // 2, t % 2, g0:g1])
+
+        def w1_quantise(t, m0, m1):
             nc.vector.quantize_mx(
-                out=w1_codes[:, t, :].bitcast(FP8X4),
-                scales=w1_scales[:, t, :],
-                in_=w1_grp[t].rearrange("p m j -> p (m j)"),
+                out=w1_codes[:, t, m0:m1].bitcast(FP8X4),
+                scales=w1_scales[:, t, m0:m1],
+                in_=w1_grp[:, t, m0:m1].rearrange("p m j -> p (m j)"),
             )
-            pieces = [(0, P, 7), (P, T - P, 0), (T - P, T, 1)] if t == 0 else [(0, T, (t + 1) % 4)]
+
+        w1_round(nc.vector.tensor_copy, 0, 0, 8)
+        w1_round(nc.vector.tensor_copy, 0, 8, 12)
+        w1_round(nc.scalar.copy, 0, 12, 16)
+        w1_round(nc.scalar.copy, 3, 0, 16)
+        w1_quantise(0, 0, P // 2)
+        w1_quantise(0, P // 2, P)
+        for t in range(PACK):
+            if t in (1, 2):
+                w1_round(nc.vector.tensor_copy, t, 0, 16)
+            if t > 0:
+                w1_quantise(t, 0, P)
+            pieces = [(0, HALF, 7), (HALF, T - P, 0), (T - P, T, 1)] if t == 0 else [(0, T, (t + 1) % 4)]
             for a, b, n_bank in pieces:
                 acc = bank(n_bank, [P, b - a], "h_acc%d_%d" % (t, a))
                 nc.tensor.matmul_mx(
@@ -104,7 +112,7 @@ def tile_picked_wpna_none_l_kernel(
                     start=True,
                     stop=True,
                 )
-                if b == P:
+                if b == HALF:
                     nc.vector.tensor_copy(out=h[t][:, a:b], in_=acc[:])
                 elif t == PACK - 1:
                     nc.scalar.activation(h[t][:, a:b], acc[:], COPY, scale=unit[:, 0:1])
@@ -143,21 +151,19 @@ def tile_picked_wpna_none_l_kernel(
                         start=(d == 0 and t == 0),
                         stop=(d == 2 and t == PACK - 1),
                     )
-            gb = sb.tile([P, v1 - v0, PACK], BF16, name="gb%d_%d" % (d, v0), align_bytes=64,
-                tag="stage0_1" if v0 == HALF else "gb%d" % d)
-            interleave(gb[:], g[:])
-            return gb
+            return g
 
-        gb0 = gather(0, 0, T)
-        gb1 = gather(1, 0, T)
-        gb2 = []
-        z_mean = []
-        for c in range(2):
-            v0 = c * HALF
-            gb2.append(gather(2, v0, v0 + HALF))
+        def rounded(g, a, b, tag):
+            gb = sb.tile([P, b - a, PACK], BF16, name="gb_" + tag, tag=tag, align_bytes=64)
+            interleave(gb[:], g[:, :, a:b])
+            return gb[:].rearrange("p v t -> p (v t)")
+
+        def mean(c):
             words = bank(c, [P, 2, 2, P], "words%d" % c)
             for bb in range(2):
-                mean_t = sb.tile([P, 2, P, 2], BF16, name="mean_t%d_%d" % (c, bb), tag="stage%d_%d" % (c, bb), align_bytes=64)
+                mean_t = sb.tile(
+                    [P, 2, P, 2], BF16, name="mean_t%d_%d" % (c, bb), tag="stage%d_%d" % (c, bb), align_bytes=64
+                )
                 nc.scalar.activation(
                     mean_t[:],
                     sums[2 * c + bb][:].rearrange("v (u e) p -> v u p e", e=2),
@@ -172,7 +178,16 @@ def tile_picked_wpna_none_l_kernel(
                 out=zm[:].bitcast(F32).rearrange("p (b v u) -> p b v u", b=2, u=2),
                 in_=words[:].rearrange("p b u v -> p b v u"),
             )
-            z_mean.append(zm)
+            return zm
+
+        first = rounded(gather(0, 0, T), 0, T, "first")
+        second = rounded(gather(1, 0, T), 0, T, "second")
+        third = {0: rounded(gather(2, 0, HALF), 0, HALF, "third")}
+        z_mean = [mean(0)]
+        g_last = gather(2, HALF, T)
+        third[HALF] = rounded(g_last, 0, P, "stage0_1")
+        z_mean.append(mean(1))
+        third[T - P] = rounded(g_last, P, HALF, "stage1_1")
 
         wz_codes = sb.tile([P, 3, N], U32, name="wz_codes", align_bytes=64)
         wz_scales = sb.tile([P, 3, N], U8, name="wz_scales", align_bytes=64)
@@ -185,67 +200,51 @@ def tile_picked_wpna_none_l_kernel(
 
         hi01 = sb.tile([P, T * PACK], BF16, name="hi01")
         lo01 = sb.tile([P, T * PACK], BF16, name="lo01")
-        flat0 = gb0[:].rearrange("p v t -> p (v t)")
-        flat1 = gb1[:].rearrange("p v t -> p (v t)")
-        nc.vector.tensor_tensor(hi01[:], flat0, flat1, MAX)
-        nc.vector.tensor_tensor(lo01[:], flat0, flat1, MIN)
+        nc.vector.tensor_tensor(hi01[:], first, second, MAX)
+        nc.vector.tensor_tensor(lo01[:], first, second, MIN)
 
-        out_rows = out.rearrange("(mt p) v -> p mt v", p=P)
-        for c in range(2):
-            cols = slice(c * HALF * PACK, (c + 1) * HALF * PACK)
-            flat2 = gb2[c][:].rearrange("p v t -> p (v t)")
-            z_max = sb.tile([P, HALF * PACK], BF16, name="z_max%d" % c, align_bytes=64)
-            z_min = sb.tile([P, HALF * PACK], BF16, name="z_min%d" % c, align_bytes=64)
-            nc.vector.tensor_tensor(z_max[:], hi01[:, cols], flat2, MAX)
-            nc.vector.tensor_tensor(z_min[:], lo01[:, cols], flat2, MIN)
-            quantised = {}
-            for s, z in ((1, z_max), (2, z_min), (0, z_mean[c])):
-                codes = sb.tile([P, HALF], U32, name="z_codes%d_%d" % (c, s), align_bytes=64)
-                scales = sb.tile([P, HALF], U8, name="z_scales%d_%d" % (c, s), align_bytes=64)
-                quantised[s] = (z, codes, scales)
+        z_codes = sb.tile([P, 3, T], U32, name="z_codes", align_bytes=64)
+        z_scales = sb.tile([P, 3, T], U8, name="z_scales", align_bytes=64)
 
-            def quantise(s, a, b):
-                z, codes, scales = quantised[s]
-                nc.vector.quantize_mx(
-                    out=codes[:, a:b].bitcast(FP8X4), scales=scales[:, a:b], in_=z[:, a * PACK : b * PACK]
-                )
+        def quantise(s, a, b, z):
+            nc.vector.quantize_mx(out=z_codes[:, s, a:b].bitcast(FP8X4), scales=z_scales[:, s, a:b], in_=z)
 
-            def product(acc, s, mt, a, b):
-                z, codes, scales = quantised[s]
+        def products(accs, s, a, b, order):
+            for mt in range(2):
                 nc.tensor.matmul_mx(
-                    out=acc[:],
+                    out=accs[mt][:],
                     lhsT=wz_codes[:, s, mt * P : (mt + 1) * P].bitcast(FP8X4),
                     lhsT_scale=wz_scales[:, s, mt * P : (mt + 1) * P],
-                    rhs=codes[:, a:b].bitcast(FP8X4),
-                    rhs_scale=scales[:, a:b],
-                    start=(s == 1),
-                    stop=(s == 0),
+                    rhs=z_codes[:, s, a:b].bitcast(FP8X4),
+                    rhs_scale=z_scales[:, s, a:b],
+                    start=(s == order[0]),
+                    stop=(s == order[-1]),
                 )
 
-            pieces = [(0, HALF)] if c == 0 else [(0, P), (P, HALF)]
-            accs = {}
-            for n_piece, (a, b) in enumerate(pieces):
-                for mt in range(2):
-                    accs[a, mt] = bank(2 + 2 * (c + n_piece) + mt, [P, b - a], "o_acc%d_%d_%d" % (c, a, mt))
-            for s in (1, 2):
-                quantise(s, 0, HALF)
-                for a, b in pieces:
-                    for mt in range(2):
-                        product(accs[a, mt], s, mt, a, b)
-            for a, b in pieces:
-                quantise(0, a, b)
-                for mt in range(2):
-                    product(accs[a, mt], 0, mt, a, b)
-                if c == 0:
-                    for mt in range(2):
-                        res = sb.tile([P, HALF], F32, name="res_first%d" % mt, tag="stage1_%d" % mt, align_bytes=64)
-                        nc.scalar.copy(out=res[:], in_=accs[a, mt][:])
-                        nc.sync.dma_start(out=out_rows[:, mt, :HALF], in_=res[:])
+        out_rows = out.rearrange("(mt p) v -> p mt v", p=P)
+        for n_piece, (a, b) in enumerate(((0, HALF), (HALF, T - P), (T - P, T))):
+            last = b == T
+            order = (0, 1, 2) if last else (1, 2, 0)
+            accs = [bank(2 + 2 * n_piece + mt, [P, b - a], "o_acc%d_%d" % (a, mt)) for mt in range(2)]
+            cols = slice(a * PACK, b * PACK)
+            z_max = sb.tile([P, (b - a) * PACK], BF16, name="z_max%d" % a, align_bytes=64)
+            z_min = sb.tile([P, (b - a) * PACK], BF16, name="z_min%d" % a, align_bytes=64)
+            nc.vector.tensor_tensor(z_max[:], hi01[:, cols], third[a], MAX)
+            nc.vector.tensor_tensor(z_min[:], lo01[:, cols], third[a], MIN)
+            if last:
+                products(accs, 0, a, b, order)
+            for s, z in ((1, z_max), (2, z_min)):
+                quantise(s, a, b, z[:])
+                products(accs, s, a, b, order)
+            if not last:
+                quantise(0, a, a + HALF, z_mean[n_piece][:])
+                products(accs, 0, a, b, order)
+            res = sb.tile([P, 2, b - a], F32, name="res%d" % a, tag="stage1_0" if a == 0 else "res%d" % a, align_bytes=64)
+            for mt in range(2):
+                if last:
+                    nc.vector.tensor_copy(out=res[:, mt, :], in_=accs[mt][:])
+                    nc.sync.dma_start(out=out_rows[:, mt, a:b], in_=res[:, mt, :])
                 else:
-                    res = sb.tile([P, 2, P], F32, name="res_last%d" % a)
-                    nc.scalar.copy(out=res[:, 0, :], in_=accs[a, 0][:])
-                    if a == 0:
-                        nc.scalar.copy(out=res[:, 1, :], in_=accs[a, 1][:])
-                    else:
-                        nc.vector.tensor_copy(out=res[:, 1, :], in_=accs[a, 1][:])
-                    nc.sync.dma_start(out=out_rows[:, :, HALF + a : HALF + b], in_=res[:])
+                    nc.scalar.copy(out=res[:, mt, :], in_=accs[mt][:])
+            if not last:
+                nc.sync.dma_start(out=out_rows[:, :, a:b], in_=res[:])

@@ -38,8 +38,10 @@ def tile_picked_wpna_none_l_kernel(
         def bank(b, shape, name):
             return ps.tile(shape, F32, name=name, tag="bank%d" % b)
 
-        w1_raw = sb.tile([P, PACK, H], F32, name="w1_raw")
-        nc.sync.dma_start(out=w1_raw[:], in_=w1.rearrange("(p j) c -> p j c", j=PACK))
+        w1_rows = w1.rearrange("(p s j) c -> s p j c", s=2, j=2)
+        w1_raw = [sb.tile([P, 2, H], F32, name="w1_raw%d" % s) for s in range(2)]
+        for s in range(2):
+            nc.sync.dma_start(out=w1_raw[s][:], in_=w1_rows[s])
         xw = sb.tile([P, 2 * T], U8, name="xw", align_bytes=64)
         nc.sync.dma_start(out=xw[:].bitcast(I32), in_=x_words[0].bitcast(I32))
         xs = sb.tile([P, T], U8, name="xs", align_bytes=64)
@@ -61,26 +63,44 @@ def tile_picked_wpna_none_l_kernel(
                 nc.sync.dma_start(out=raw[:, 2 * u : 2 * u + 2, :].rearrange("p e c -> p (e c)"), in_=rows[u])
             wz_raw.append(raw)
 
+        warm_in = sb.tile([P, PACK * (HALF + P)], BF16, name="warm_in", align_bytes=64)
+        nc.gpsimd.memset(warm_in[:].bitcast(I32), 0)
         ident = sb.tile([P, P], F32, name="ident")
         make_identity(nc, ident[:])
 
-        zeros = sb.tile([P, WINDOW - T], F32, name="zeros")
-        nc.vector.memset(zeros[:], 0.0)
         plane_bytes = 4 * PACK * T
         unit = late.tile([P, PACK * HALF + 16], F32, name="unit", offset=plane_bytes - 32)
         nc.vector.memset(unit[:, 0:1], 1.0)
         h = [sb.tile([P, WINDOW], F32, name="h%d" % t) for t in range(PACK)]
+        warm_codes = sb.tile([P, HALF + P], U32, name="warm_codes", align_bytes=64)
+        warm_scales = sb.tile([P, HALF + P], U8, name="warm_scales", align_bytes=64)
+        nc.vector.quantize_mx(out=warm_codes[:, :HALF].bitcast(FP8X4), scales=warm_scales[:, :HALF], in_=warm_in[:, : PACK * HALF])
+        nc.scalar.activation(warm_in[:, PACK * HALF : PACK * HALF + 16], warm_in[:, :16], COPY)
         for t in range(PACK):
-            nc.scalar.activation(h[t][:, T:], zeros[:], COPY)
+            nc.scalar.activation(h[t][:, T:], warm_in[:].bitcast(F32)[:, : WINDOW - T], COPY)
+        nc.vector.quantize_mx(out=warm_codes[:, HALF:].bitcast(FP8X4), scales=warm_scales[:, HALF:], in_=warm_in[:, PACK * HALF :])
+        for n_bank in range(2, 7):
+            warm = bank(n_bank, [P, HALF], "warm%d" % n_bank)
+            nc.tensor.matmul_mx(
+                out=warm[:],
+                lhsT=warm_codes[:, HALF:].bitcast(FP8X4),
+                lhsT_scale=warm_scales[:, HALF:],
+                rhs=warm_codes[:, :HALF].bitcast(FP8X4),
+                rhs_scale=warm_scales[:, :HALF],
+                start=True,
+                stop=True,
+            )
 
         w1_grp = sb.tile([P, PACK, P, PACK], BF16, name="w1_grp", align_bytes=64)
-        w1_from = w1_raw[:].rearrange("p j (g u a i e) -> p u e g a j i", u=2, a=RUN // LINE, i=LINE, e=2)
-        w1_into = w1_grp[:].rearrange("p t (g a i) j -> p t g a j i", a=RUN // LINE, i=LINE)
+        w1_from = [
+            raw[:].rearrange("p j (g u a i e) -> p u e g a j i", u=2, a=RUN // LINE, i=LINE, e=2) for raw in w1_raw
+        ]
+        w1_into = w1_grp[:].rearrange("p t (g a i) (s j) -> p s t g a j i", a=RUN // LINE, i=LINE, s=2)
         w1_codes = sb.tile([P, PACK, P], U32, name="w1_codes", align_bytes=64)
         w1_scales = sb.tile([P, PACK, P], U8, name="w1_scales", align_bytes=64)
 
-        def w1_round(copy, t, g0, g1):
-            copy(out=w1_into[:, t, g0:g1], in_=w1_from[:, t // 2, t % 2, g0:g1])
+        def w1_round(copy, s, t, g0, g1):
+            copy(out=w1_into[:, s, t, g0:g1], in_=w1_from[s][:, t // 2, t % 2, g0:g1])
 
         def w1_quantise(t, m0, m1):
             nc.vector.quantize_mx(
@@ -89,15 +109,17 @@ def tile_picked_wpna_none_l_kernel(
                 in_=w1_grp[:, t, m0:m1].rearrange("p m j -> p (m j)"),
             )
 
-        w1_round(nc.vector.tensor_copy, 0, 0, 8)
-        w1_round(nc.vector.tensor_copy, 0, 8, 12)
-        w1_round(nc.scalar.copy, 0, 12, 16)
-        w1_round(nc.scalar.copy, 3, 0, 16)
+        for t in range(PACK):
+            w1_round(nc.vector.tensor_copy if t < 3 else nc.scalar.copy, 0, t, 0, 16)
+        w1_round(nc.vector.tensor_copy, 1, 0, 0, 8)
+        w1_round(nc.vector.tensor_copy, 1, 0, 8, 16)
+        w1_round(nc.scalar.copy, 1, 2, 0, 16)
+        w1_round(nc.scalar.copy, 1, 3, 0, 16)
         w1_quantise(0, 0, P // 2)
         w1_quantise(0, P // 2, P)
         for t in range(PACK):
-            if t in (1, 2):
-                w1_round(nc.vector.tensor_copy, t, 0, 16)
+            if t == 1:
+                w1_round(nc.vector.tensor_copy, 1, t, 0, 16)
             if t > 0:
                 w1_quantise(t, 0, P)
             pieces = [(0, HALF, 7), (HALF, T - P, 0), (T - P, T, 1)] if t == 0 else [(0, T, (t + 1) % 4)]
@@ -125,11 +147,9 @@ def tile_picked_wpna_none_l_kernel(
                 in_=src.rearrange("p t (c i) -> p c t i", i=LINE),
             )
 
-        wz_grp = []
+        wz_grp = sb.tile([P, 3, N, PACK], BF16, name="wz_grp", align_bytes=64)
         for s in range(3):
-            grp = sb.tile([P, N, PACK], BF16, name="wz_grp%d" % s, align_bytes=64)
-            interleave(grp[:], wz_raw[s][:])
-            wz_grp.append(grp)
+            interleave(wz_grp[:, s], wz_raw[s][:])
 
         sums = [bank(4 + b, [P, PACK, P], "sum%d" % b) for b in range(T // P)]
 
@@ -191,11 +211,11 @@ def tile_picked_wpna_none_l_kernel(
 
         wz_codes = sb.tile([P, 3, N], U32, name="wz_codes", align_bytes=64)
         wz_scales = sb.tile([P, 3, N], U8, name="wz_scales", align_bytes=64)
-        for s in range(3):
+        for s0, s1 in ((0, 2), (2, 3)):
             nc.vector.quantize_mx(
-                out=wz_codes[:, s, :].bitcast(FP8X4),
-                scales=wz_scales[:, s, :],
-                in_=wz_grp[s][:].rearrange("p c j -> p (c j)"),
+                out=wz_codes[:, s0:s1].rearrange("p s c -> p (s c)").bitcast(FP8X4),
+                scales=wz_scales[:, s0:s1].rearrange("p s c -> p (s c)"),
+                in_=wz_grp[:, s0:s1].rearrange("p s c j -> p (s c j)"),
             )
 
         hi01 = sb.tile([P, T * PACK], BF16, name="hi01")

@@ -218,10 +218,11 @@ def tile_picked_wpna_none_l_kernel(
                 in_=wz_grp[:, s0:s1].rearrange("p s c j -> p (s c j)"),
             )
 
-        hi01 = sb.tile([P, T * PACK], BF16, name="hi01")
-        lo01 = sb.tile([P, T * PACK], BF16, name="lo01")
-        nc.vector.tensor_tensor(hi01[:], first, second, MAX)
-        nc.vector.tensor_tensor(lo01[:], first, second, MIN)
+        pair = late.tile([P, 2, T * PACK], BF16, name="pair", offset=plane_bytes // 2)
+
+        def pair_of(n_op, c):
+            half = slice(c * HALF * PACK, (c + 1) * HALF * PACK)
+            nc.vector.tensor_tensor(pair[:, n_op, half], first[:, half], second[:, half], (MAX, MIN)[n_op])
 
         z_codes = sb.tile([P, 3, T], U32, name="z_codes", align_bytes=64)
         z_scales = sb.tile([P, 3, T], U8, name="z_scales", align_bytes=64)
@@ -249,13 +250,18 @@ def tile_picked_wpna_none_l_kernel(
             cols = slice(a * PACK, b * PACK)
             z_max = sb.tile([P, (b - a) * PACK], BF16, name="z_max%d" % a, align_bytes=64)
             z_min = sb.tile([P, (b - a) * PACK], BF16, name="z_min%d" % a, align_bytes=64)
-            nc.vector.tensor_tensor(z_max[:], hi01[:, cols], third[a], MAX)
-            nc.vector.tensor_tensor(z_min[:], lo01[:, cols], third[a], MIN)
+            if a == 0:
+                pair_of(0, 0)
+                pair_of(1, 0)
+            nc.vector.tensor_tensor(z_max[:], pair[:, 0, cols], third[a], MAX)
+            nc.vector.tensor_tensor(z_min[:], pair[:, 1, cols], third[a], MIN)
             if last:
                 products(accs, 0, a, b, order)
             for s, z in ((1, z_max), (2, z_min)):
                 quantise(s, a, b, z[:])
                 products(accs, s, a, b, order)
+                if a == 0:
+                    pair_of(s - 1, 1)
             if not last:
                 quantise(0, a, a + HALF, z_mean[n_piece][:])
                 products(accs, 0, a, b, order)

@@ -17,6 +17,9 @@ FP4X4 = mybir.dt.float4_e2m1fn_x4
 COPY = mybir.ActivationFunctionType.Copy
 MAX = mybir.AluOpType.max
 MIN = mybir.AluOpType.min
+ADD = mybir.AluOpType.add
+SUB = mybir.AluOpType.subtract
+RELU = mybir.ActivationFunctionType.Relu
 
 P = 128
 PACK = 4
@@ -68,8 +71,8 @@ def tile_picked_wpna_none_l_kernel(
         ident = sb.tile([P, P], F32, name="ident")
         make_identity(nc, ident[:])
 
-        plane_bytes = 4 * PACK * T
-        unit = late.tile([P, PACK * HALF + 16], F32, name="unit", offset=plane_bytes - 32)
+        half_bytes = 4 * PACK * HALF
+        unit = late.tile([P, 2 * PACK * HALF + 16], F32, name="unit", offset=half_bytes - 32)
         nc.vector.memset(unit[:, 0:1], 1.0)
         h = [sb.tile([P, WINDOW], F32, name="h%d" % t) for t in range(PACK)]
         warm_codes = sb.tile([P, HALF + P], U32, name="warm_codes", align_bytes=64)
@@ -151,26 +154,24 @@ def tile_picked_wpna_none_l_kernel(
         for s in range(3):
             interleave(wz_grp[:, s], wz_raw[s][:])
 
-        sums = [bank(4 + b, [P, PACK, P], "sum%d" % b) for b in range(T // P)]
+        sums = [[bank(4 + 2 * u + c, [P, 2, 2, P], "sum%d_%d" % (u, c)) for c in range(2)] for u in range(2)]
 
-        def gather(d, v0, v1):
-            if d == 0:
-                g = sb.tile([P, PACK, v1 - v0], F32, name="g0")
-            else:
-                g = late.tile(
-                    [P, PACK, v1 - v0], F32, name="g%d_%d" % (d, v0), offset=(d - 1) * plane_bytes + 4 * PACK * v0
+        def gather(d, g, t, v0):
+            nc.vector.tensor_copy(g[:, t, :], h[t][:].indirect(lists[d][:, v0 // 16 : (v0 + HALF) // 16]))
+            for b in range(v0 // P, (v0 + HALF) // P):
+                nc.tensor.matmul(
+                    sums[t // 2][b // 2][:, b % 2, t % 2, :],
+                    lhsT=g[:, t, b * P - v0 : (b + 1) * P - v0],
+                    rhs=ident[:],
+                    is_transpose=True,
+                    start=(d == 0 and t % 2 == 0 and b % 2 == 0),
+                    stop=(d == 2 and t % 2 == 1 and b % 2 == 1),
                 )
+
+        def gather_late(d, v0, slot):
+            g = late.tile([P, PACK, HALF], F32, name="g%d_%d" % (d, v0), offset=slot * half_bytes)
             for t in range(PACK):
-                nc.vector.tensor_copy(g[:, t, :], h[t][:].indirect(lists[d][:, v0 // 16 : v1 // 16]))
-                for b in range(v0 // P, v1 // P):
-                    nc.tensor.matmul(
-                        sums[b][:, t, :],
-                        lhsT=g[:, t, b * P - v0 : (b + 1) * P - v0],
-                        rhs=ident[:],
-                        is_transpose=True,
-                        start=(d == 0 and t == 0),
-                        stop=(d == 2 and t == PACK - 1),
-                    )
+                gather(d, g, t, v0)
             return g
 
         def rounded(g, a, b, tag):
@@ -178,36 +179,63 @@ def tile_picked_wpna_none_l_kernel(
             interleave(gb[:], g[:, :, a:b])
             return gb[:].rearrange("p v t -> p (v t)")
 
-        def mean(c):
-            words = bank(c, [P, 2, 2, P], "words%d" % c)
+        words = [bank(c, [P, 2, 2, P], "words%d" % c) for c in range(2)]
+        held = 5 * half_bytes
+        stage = [[held + 64 + 1024 * (2 * u + c) for c in range(2)] for u in range(2)]
+
+        def round_third(g, a, b, name, offset):
+            gb = late.tile([P, b - a, PACK], BF16, name=name, offset=offset)
+            interleave(gb[:], g[:, :, a:b])
+            return gb[:].rearrange("p v t -> p (v t)")
+
+        def mean_turn(u, c):
+            mean_t = late.tile([P, 2, P, 2], BF16, name="mean_t%d_%d" % (u, c), offset=stage[u][c])
+            nc.scalar.activation(mean_t[:], sums[u][c][:].rearrange("v b e p -> v b p e"), COPY, scale=1.0 / 3.0)
+            turned = mean_t[:].rearrange("v b p e -> v (b p e)").bitcast(F32)
             for bb in range(2):
-                mean_t = sb.tile(
-                    [P, 2, P, 2], BF16, name="mean_t%d_%d" % (c, bb), tag="stage%d_%d" % (c, bb), align_bytes=64
-                )
-                nc.scalar.activation(
-                    mean_t[:],
-                    sums[2 * c + bb][:].rearrange("v (u e) p -> v u p e", e=2),
-                    COPY,
-                    scale=1.0 / 3.0,
-                )
-                pairs = mean_t[:].rearrange("v u p e -> v (u p e)").bitcast(F32)
-                for u in range(2):
-                    nc.tensor.transpose(words[:, bb, u, :], pairs[:, u * P : (u + 1) * P], ident[:])
+                nc.tensor.transpose(words[c][:, bb, u, :], turned[:, bb * P : (bb + 1) * P], ident[:])
+
+        def mean_out(c):
             zm = sb.tile([P, HALF * PACK], BF16, name="z_mean%d" % c, align_bytes=64)
             nc.scalar.copy(
                 out=zm[:].bitcast(F32).rearrange("p (b v u) -> p b v u", b=2, u=2),
-                in_=words[:].rearrange("p b u v -> p b v u"),
+                in_=words[c][:].rearrange("p b u v -> p b v u"),
             )
             return zm
 
-        first = rounded(gather(0, 0, T), 0, T, "first")
-        second = rounded(gather(1, 0, T), 0, T, "second")
-        third = {0: rounded(gather(2, 0, HALF), 0, HALF, "third")}
-        z_mean = [mean(0)]
-        g_last = gather(2, HALF, T)
-        third[HALF] = rounded(g_last, 0, P, "stage0_1")
-        z_mean.append(mean(1))
-        third[T - P] = rounded(g_last, P, HALF, "stage1_1")
+        early = [sb.tile([P, PACK, HALF], F32, name="early%d" % d) for d in range(2)]
+        excess = sb.tile([P, PACK, HALF], F32, name="excess")
+        for u in range(2):
+            for t in (2 * u, 2 * u + 1):
+                for d in range(2):
+                    gather(d, early[d], t, HALF)
+            diff = sb.tile([P, 2, HALF], F32, name="diff%d" % u)
+            nc.gpsimd.tensor_tensor(diff[:], early[1][:, 2 * u : 2 * u + 2], early[0][:, 2 * u : 2 * u + 2], SUB)
+            nc.scalar.activation(excess[:, 2 * u : 2 * u + 2], diff[:], RELU)
+        ends = []
+        for n_op in range(2):
+            gb = sb.tile([P, HALF, PACK], BF16, name="end%d" % n_op, align_bytes=64)
+            nc.gpsimd.tensor_tensor(
+                gb[:].rearrange("p (c i) t -> p c t i", i=LINE),
+                early[n_op][:].rearrange("p t (c i) -> p c t i", i=LINE),
+                excess[:].rearrange("p t (c i) -> p c t i", i=LINE),
+                (ADD, SUB)[n_op],
+            )
+            ends.append(gb[:].rearrange("p v t -> p (v t)"))
+        larger, smaller = ends
+        first = rounded(gather_late(0, 0, 0), 0, HALF, "first")
+        second = rounded(gather_late(1, 0, 1), 0, HALF, "second")
+        g_third = gather_late(2, 0, 2)
+        mean_turn(0, 0)
+        third = {0: round_third(g_third, 0, HALF, "third0", held + 64 - 2048)}
+        mean_turn(1, 0)
+        g_last = gather_late(2, HALF, 3)
+        for u in range(2):
+            mean_turn(u, 1)
+        z_mean = [mean_out(0)]
+        third[HALF] = round_third(g_last, 0, P, "third1", stage[1][0] - 512)
+        z_mean.append(mean_out(1))
+        third[T - P] = round_third(g_last, P, HALF, "third2", stage[1][1] - 480)
 
         wz_codes = sb.tile([P, 3, N], U32, name="wz_codes", align_bytes=64)
         wz_scales = sb.tile([P, 3, N], U8, name="wz_scales", align_bytes=64)
@@ -218,13 +246,12 @@ def tile_picked_wpna_none_l_kernel(
                 in_=wz_grp[:, s0:s1].rearrange("p s c j -> p (s c j)"),
             )
 
-        pair = late.tile([P, 2, T * PACK], BF16, name="pair", offset=plane_bytes // 2)
+        pair = sb.tile([P, 2, HALF * PACK], BF16, name="pair")
+        for n_op in range(2):
+            nc.vector.tensor_tensor(pair[:, n_op], first, second, (MAX, MIN)[n_op])
+        pairs = [(pair[:, 0], pair[:, 1]), (larger, smaller)]
 
-        def pair_of(n_op, c):
-            half = slice(c * HALF * PACK, (c + 1) * HALF * PACK)
-            nc.vector.tensor_tensor(pair[:, n_op, half], first[:, half], second[:, half], (MAX, MIN)[n_op])
-
-        z_codes = sb.tile([P, 3, T], U32, name="z_codes", align_bytes=64)
+        z_codes = late.tile([P, 3, T], U32, name="z_codes", offset=held + 3712, align_bytes=64)
         z_scales = sb.tile([P, 3, T], U8, name="z_scales", align_bytes=64)
 
         def quantise(s, a, b, z):
@@ -247,25 +274,20 @@ def tile_picked_wpna_none_l_kernel(
             last = b == T
             order = (0, 1, 2) if last else (1, 2, 0)
             accs = [bank(2 + 2 * n_piece + mt, [P, b - a], "o_acc%d_%d" % (a, mt)) for mt in range(2)]
-            cols = slice(a * PACK, b * PACK)
+            cols = slice(a % HALF * PACK, a % HALF * PACK + (b - a) * PACK)
             z_max = sb.tile([P, (b - a) * PACK], BF16, name="z_max%d" % a, align_bytes=64)
             z_min = sb.tile([P, (b - a) * PACK], BF16, name="z_min%d" % a, align_bytes=64)
-            if a == 0:
-                pair_of(0, 0)
-                pair_of(1, 0)
-            nc.vector.tensor_tensor(z_max[:], pair[:, 0, cols], third[a], MAX)
-            nc.vector.tensor_tensor(z_min[:], pair[:, 1, cols], third[a], MIN)
+            nc.vector.tensor_tensor(z_max[:], pairs[a // HALF][0][:, cols], third[a], MAX)
+            nc.vector.tensor_tensor(z_min[:], pairs[a // HALF][1][:, cols], third[a], MIN)
             if last:
                 products(accs, 0, a, b, order)
             for s, z in ((1, z_max), (2, z_min)):
                 quantise(s, a, b, z[:])
                 products(accs, s, a, b, order)
-                if a == 0:
-                    pair_of(s - 1, 1)
             if not last:
                 quantise(0, a, a + HALF, z_mean[n_piece][:])
                 products(accs, 0, a, b, order)
-            res = sb.tile([P, 2, b - a], F32, name="res%d" % a, tag="stage1_0" if a == 0 else "res%d" % a, align_bytes=64)
+            res = sb.tile([P, 2, b - a], F32, name="res%d" % a, align_bytes=64)
             for mt in range(2):
                 if last:
                     nc.vector.tensor_copy(out=res[:, mt, :], in_=accs[mt][:])

@@ -66,7 +66,7 @@ def tile_picked_wpna_none_l_kernel(
                 nc.sync.dma_start(out=raw[:, 2 * u : 2 * u + 2, :].rearrange("p e c -> p (e c)"), in_=rows[u])
             wz_raw.append(raw)
 
-        warm_in = sb.tile([P, PACK * (HALF + P)], BF16, name="warm_in", align_bytes=64)
+        warm_in = sb.tile([P, 2 * (WINDOW - T)], BF16, name="warm_in", align_bytes=64)
         nc.gpsimd.memset(warm_in[:].bitcast(I32), 0)
         ident = sb.tile([P, P], F32, name="ident")
         make_identity(nc, ident[:])
@@ -75,24 +75,8 @@ def tile_picked_wpna_none_l_kernel(
         unit = late.tile([P, 2 * PACK * HALF + 16], F32, name="unit", offset=half_bytes - 32)
         nc.vector.memset(unit[:, 0:1], 1.0)
         h = [sb.tile([P, WINDOW], F32, name="h%d" % t) for t in range(PACK)]
-        warm_codes = sb.tile([P, HALF + P], U32, name="warm_codes", align_bytes=64)
-        warm_scales = sb.tile([P, HALF + P], U8, name="warm_scales", align_bytes=64)
-        nc.vector.quantize_mx(out=warm_codes[:, :HALF].bitcast(FP8X4), scales=warm_scales[:, :HALF], in_=warm_in[:, : PACK * HALF])
-        nc.scalar.activation(warm_in[:, PACK * HALF : PACK * HALF + 16], warm_in[:, :16], COPY)
         for t in range(PACK):
             nc.scalar.activation(h[t][:, T:], warm_in[:].bitcast(F32)[:, : WINDOW - T], COPY)
-        nc.vector.quantize_mx(out=warm_codes[:, HALF:].bitcast(FP8X4), scales=warm_scales[:, HALF:], in_=warm_in[:, PACK * HALF :])
-        for n_bank in range(2, 7):
-            warm = bank(n_bank, [P, HALF], "warm%d" % n_bank)
-            nc.tensor.matmul_mx(
-                out=warm[:],
-                lhsT=warm_codes[:, HALF:].bitcast(FP8X4),
-                lhsT_scale=warm_scales[:, HALF:],
-                rhs=warm_codes[:, :HALF].bitcast(FP8X4),
-                rhs_scale=warm_scales[:, :HALF],
-                start=True,
-                stop=True,
-            )
 
         w1_grp = sb.tile([P, PACK, P, PACK], BF16, name="w1_grp", align_bytes=64)
         w1_from = [

@@ -15,18 +15,35 @@ U8 = mybir.dt.uint8
 FP8X4 = mybir.dt.float8_e4m3fn_x4
 FP4X4 = mybir.dt.float4_e2m1fn_x4
 COPY = mybir.ActivationFunctionType.Copy
+RELU = mybir.ActivationFunctionType.Relu
 MAX = mybir.AluOpType.max
 MIN = mybir.AluOpType.min
 ADD = mybir.AluOpType.add
 SUB = mybir.AluOpType.subtract
-RELU = mybir.ActivationFunctionType.Relu
 
 P = 128
 PACK = 4
-WINDOW = 704
 LINE = 4
 RUN = 8
 HALF = T // 2
+
+KIB = 1024
+GATHERED = 4 * KIB
+THIRD_FIRST_AT = 64
+STAGED_AT = THIRD_FIRST_AT + 2 * KIB
+THIRD_MIDDLE_AT = STAGED_AT + 2 * KIB - 512
+THIRD_LAST_AT = STAGED_AT + 3 * KIB - 480
+Z_CODES_AT = STAGED_AT + 3 * KIB + 576
+PAIR_LISTS_AT = 12 * KIB
+W2_RAW_AT = PAIR_LISTS_AT + GATHERED // 2
+THIRD_LIST_AT = PAIR_LISTS_AT + 2 * GATHERED
+DIFF_FIRST_AT = THIRD_LIST_AT + GATHERED - KIB
+W3_RAW_AT = 32 * KIB
+W4_RAW_AT = 36 * KIB
+PAIR_ROUNDED_AT = 44 * KIB
+DIFF_LAST_AT = PAIR_ROUNDED_AT - KIB
+PLANE_AT = (56 * KIB, 58 * KIB, 50 * KIB, 48 * KIB)
+W34_CODES_AT = PLANE_AT[2]
 
 
 def tile_picked_wpna_none_l_kernel(
@@ -35,11 +52,23 @@ def tile_picked_wpna_none_l_kernel(
     nc = tc.nc
     with ExitStack() as ctx:
         sb = ctx.enter_context(tc.tile_pool(name="sb", bufs=1))
-        late = ctx.enter_context(tc.tile_pool(name="late", bufs=1))
+        shared = ctx.enter_context(tc.tile_pool(name="shared", bufs=1))
         ps = ctx.enter_context(tc.psum_pool(name="ps", bufs=1))
 
-        def bank(b, shape, name):
-            return ps.tile(shape, F32, name=name, tag="bank%d" % b)
+        def bank(n_bank, shape, name):
+            return ps.tile(shape, F32, name=name, tag="bank%d" % n_bank)
+
+        def lines(planes):
+            return planes.rearrange("p t (c i) -> p c t i", i=LINE)
+
+        def woven(words):
+            return words.rearrange("p (c i) t -> p c t i", i=LINE)
+
+        def flat(words):
+            return words.rearrange("p v t -> p (v t)")
+
+        def interleave(dst, src):
+            nc.scalar.copy(out=woven(dst), in_=lines(src))
 
         w1_rows = w1.rearrange("(p s j) c -> s p j c", s=2, j=2)
         w1_raw = [sb.tile([P, 2, H], F32, name="w1_raw%d" % s) for s in range(2)]
@@ -54,30 +83,20 @@ def tile_picked_wpna_none_l_kernel(
                 out=xs[32 * q : 32 * q + 4, :].bitcast(I32), in_=x_scales[0, 4 * q : 4 * q + 4, :].bitcast(I32)
             )
         lists = [sb.tile([P, T // 16], U16, name="pos%d" % d) for d in range(3)]
-        nc.sync.dma_start(lists[0][:], pos1)
+        for tile, pos in zip(lists, (pos1, pos2, pos3)):
+            nc.sync.dma_start(tile[:], pos)
         wz_raw = []
-        for s, w in enumerate((w2, w3, w4)):
-            raw = sb.tile([P, PACK, N], F32, name="wz_raw%d" % s)
-            if s == 0:
-                nc.sync.dma_start(lists[1][:], pos2)
-                nc.sync.dma_start(lists[2][:], pos3)
+        for s, (w, at) in enumerate(((w2, W2_RAW_AT), (w3, W3_RAW_AT), (w4, W4_RAW_AT))):
+            raw = shared.tile([P, PACK, N], F32, name="wz_raw%d" % s, offset=at)
             rows = w.rearrange("(g u r e) c -> u g r (e c)", u=2, r=RUN, e=2)
             for u in range(2):
                 nc.sync.dma_start(out=raw[:, 2 * u : 2 * u + 2, :].rearrange("p e c -> p (e c)"), in_=rows[u])
             wz_raw.append(raw)
 
-        warm_in = sb.tile([P, 2 * (WINDOW - T)], BF16, name="warm_in", align_bytes=64)
-        nc.gpsimd.memset(warm_in[:].bitcast(I32), 0)
         ident = sb.tile([P, P], F32, name="ident")
         make_identity(nc, ident[:])
 
-        half_bytes = 4 * PACK * HALF
-        unit = late.tile([P, 2 * PACK * HALF + 16], F32, name="unit", offset=half_bytes - 32)
-        nc.vector.memset(unit[:, 0:1], 1.0)
-        h = [sb.tile([P, WINDOW], F32, name="h%d" % t) for t in range(PACK)]
-        for t in range(PACK):
-            nc.scalar.activation(h[t][:, T:], warm_in[:].bitcast(F32)[:, : WINDOW - T], COPY)
-
+        h = [shared.tile([P, T], F32, name="h%d" % t, offset=PLANE_AT[t]) for t in range(PACK)]
         w1_grp = sb.tile([P, PACK, P, PACK], BF16, name="w1_grp", align_bytes=64)
         w1_from = [
             raw[:].rearrange("p j (g u a i e) -> p u e g a j i", u=2, a=RUN // LINE, i=LINE, e=2) for raw in w1_raw
@@ -85,8 +104,9 @@ def tile_picked_wpna_none_l_kernel(
         w1_into = w1_grp[:].rearrange("p t (g a i) (s j) -> p s t g a j i", a=RUN // LINE, i=LINE, s=2)
         w1_codes = sb.tile([P, PACK, P], U32, name="w1_codes", align_bytes=64)
         w1_scales = sb.tile([P, PACK, P], U8, name="w1_scales", align_bytes=64)
+        groups = P // RUN
 
-        def w1_round(copy, s, t, g0, g1):
+        def w1_round(copy, s, t, g0=0, g1=groups):
             copy(out=w1_into[:, s, t, g0:g1], in_=w1_from[s][:, t // 2, t % 2, g0:g1])
 
         def w1_quantise(t, m0, m1):
@@ -96,147 +116,134 @@ def tile_picked_wpna_none_l_kernel(
                 in_=w1_grp[:, t, m0:m1].rearrange("p m j -> p (m j)"),
             )
 
-        for t in range(PACK):
-            w1_round(nc.vector.tensor_copy if t < 3 else nc.scalar.copy, 0, t, 0, 16)
-        w1_round(nc.vector.tensor_copy, 1, 0, 0, 8)
-        w1_round(nc.vector.tensor_copy, 1, 0, 8, 16)
-        w1_round(nc.scalar.copy, 1, 2, 0, 16)
-        w1_round(nc.scalar.copy, 1, 3, 0, 16)
+        for a in range(RUN // LINE):
+            nc.scalar.activation(w1_into[:, 0, 3, :, a], w1_from[0][:, 1, 1, :, a], COPY)
+        for t in range(3):
+            w1_round(nc.vector.tensor_copy, 0, t)
+        w1_round(nc.vector.tensor_copy, 1, 0, 0, groups // 2)
+        w1_round(nc.vector.tensor_copy, 1, 0, groups // 2, groups)
+        w1_round(nc.scalar.copy, 1, 2)
+        w1_round(nc.scalar.copy, 1, 3)
         w1_quantise(0, 0, P // 2)
         w1_quantise(0, P // 2, P)
-        for t in range(PACK):
-            if t == 1:
-                w1_round(nc.vector.tensor_copy, 1, t, 0, 16)
-            if t > 0:
-                w1_quantise(t, 0, P)
-            pieces = [(0, HALF, 7), (HALF, T - P, 0), (T - P, T, 1)] if t == 0 else [(0, T, (t + 1) % 4)]
-            for a, b, n_bank in pieces:
-                acc = bank(n_bank, [P, b - a], "h_acc%d_%d" % (t, a))
-                nc.tensor.matmul_mx(
-                    out=acc[:],
-                    lhsT=w1_codes[:, t, :].bitcast(FP8X4),
-                    lhsT_scale=w1_scales[:, t, :],
-                    rhs=xw[:, 2 * a : 2 * b].bitcast(FP4X4),
-                    rhs_scale=xs[:, a:b],
-                    start=True,
-                    stop=True,
-                )
-                if b == HALF:
-                    nc.vector.tensor_copy(out=h[t][:, a:b], in_=acc[:])
-                elif t == PACK - 1:
-                    nc.scalar.activation(h[t][:, a:b], acc[:], COPY, scale=unit[:, 0:1])
-                else:
-                    nc.scalar.copy(out=h[t][:, a:b], in_=acc[:])
 
-        def interleave(dst, src):
-            nc.scalar.copy(
-                out=dst.rearrange("p (c i) t -> p c t i", i=LINE),
-                in_=src.rearrange("p t (c i) -> p c t i", i=LINE),
+        def project(t, a, b, n_bank, copy):
+            acc = bank(n_bank, [P, b - a], "h_acc%d_%d" % (t, a))
+            nc.tensor.matmul_mx(
+                out=acc[:],
+                lhsT=w1_codes[:, t, :].bitcast(FP8X4),
+                lhsT_scale=w1_scales[:, t, :],
+                rhs=xw[:, 2 * a : 2 * b].bitcast(FP4X4),
+                rhs_scale=xs[:, a:b],
+                start=True,
+                stop=True,
             )
+            copy(out=h[t][:, a:b], in_=acc[:])
 
-        wz_grp = sb.tile([P, 3, N, PACK], BF16, name="wz_grp", align_bytes=64)
-        for s in range(3):
-            interleave(wz_grp[:, s], wz_raw[s][:])
+        project(0, 0, HALF, 7, nc.vector.tensor_copy)
+        project(0, HALF, T - P, 0, nc.scalar.copy)
+        project(0, T - P, T, 1, nc.scalar.copy)
+        w1_round(nc.vector.tensor_copy, 1, 1)
+        for t, n_bank in ((1, 2), (2, 3), (3, 0)):
+            w1_quantise(t, 0, P)
+            project(t, 0, T, n_bank, nc.scalar.copy)
 
-        sums = [[bank(4 + 2 * u + c, [P, 2, 2, P], "sum%d_%d" % (u, c)) for c in range(2)] for u in range(2)]
+        sums = [[bank(4 + 2 * u + half, [P, 2, 2, P], "sum%d_%d" % (u, half)) for half in range(2)] for u in range(2)]
 
-        def gather(d, g, t, v0):
-            nc.vector.tensor_copy(g[:, t, :], h[t][:].indirect(lists[d][:, v0 // 16 : (v0 + HALF) // 16]))
-            for b in range(v0 // P, (v0 + HALF) // P):
+        def gather(d, dst, t, half):
+            nc.vector.tensor_copy(dst, h[t][:].indirect(lists[d][:, half * HALF // 16 : (half + 1) * HALF // 16]))
+            for blk in range(2):
                 nc.tensor.matmul(
-                    sums[t // 2][b // 2][:, b % 2, t % 2, :],
-                    lhsT=g[:, t, b * P - v0 : (b + 1) * P - v0],
+                    sums[t // 2][half][:, blk, t % 2, :],
+                    lhsT=dst[:, blk * P : (blk + 1) * P],
                     rhs=ident[:],
                     is_transpose=True,
-                    start=(d == 0 and t % 2 == 0 and b % 2 == 0),
-                    stop=(d == 2 and t % 2 == 1 and b % 2 == 1),
+                    start=(d == 0 and t % 2 == 0 and blk == 0),
+                    stop=(d == 2 and t % 2 == 1 and blk == 1),
                 )
 
-        def gather_late(d, v0, slot):
-            g = late.tile([P, PACK, HALF], F32, name="g%d_%d" % (d, v0), offset=slot * half_bytes)
+        def gather_list(d, half, at):
+            g = shared.tile([P, PACK, HALF], F32, name="g%d_%d" % (d, half), offset=at)
             for t in range(PACK):
-                gather(d, g, t, v0)
+                gather(d, g[:, t, :], t, half)
             return g
 
-        def rounded(g, a, b, tag):
-            gb = sb.tile([P, b - a, PACK], BF16, name="gb_" + tag, tag=tag, align_bytes=64)
-            interleave(gb[:], g[:, :, a:b])
-            return gb[:].rearrange("p v t -> p (v t)")
+        mean_words = [bank(half, [P, 2, 2, P], "mean_words%d" % half) for half in range(2)]
 
-        words = [bank(c, [P, 2, 2, P], "words%d" % c) for c in range(2)]
-        held = 5 * half_bytes
-        stage = [[held + 64 + 1024 * (2 * u + c) for c in range(2)] for u in range(2)]
+        def round_third(g, a, b, name, at):
+            rounded = shared.tile([P, b - a, PACK], BF16, name=name, offset=at)
+            interleave(rounded[:], g[:, :, a:b])
+            return flat(rounded[:])
 
-        def round_third(g, a, b, name, offset):
-            gb = late.tile([P, b - a, PACK], BF16, name=name, offset=offset)
-            interleave(gb[:], g[:, :, a:b])
-            return gb[:].rearrange("p v t -> p (v t)")
-
-        def mean_turn(u, c):
-            mean_t = late.tile([P, 2, P, 2], BF16, name="mean_t%d_%d" % (u, c), offset=stage[u][c])
-            nc.scalar.activation(mean_t[:], sums[u][c][:].rearrange("v b e p -> v b p e"), COPY, scale=1.0 / 3.0)
-            turned = mean_t[:].rearrange("v b p e -> v (b p e)").bitcast(F32)
-            for bb in range(2):
-                nc.tensor.transpose(words[c][:, bb, u, :], turned[:, bb * P : (bb + 1) * P], ident[:])
-
-        def mean_out(c):
-            zm = sb.tile([P, HALF * PACK], BF16, name="z_mean%d" % c, align_bytes=64)
-            nc.scalar.copy(
-                out=zm[:].bitcast(F32).rearrange("p (b v u) -> p b v u", b=2, u=2),
-                in_=words[c][:].rearrange("p b u v -> p b v u"),
+        def mean_turn(u, half):
+            staged = shared.tile(
+                [P, 2, P, 2], BF16, name="staged%d_%d" % (u, half), offset=STAGED_AT + KIB * (2 * u + half)
             )
-            return zm
+            nc.scalar.activation(staged[:], sums[u][half][:].rearrange("v b e p -> v b p e"), COPY, scale=1.0 / 3.0)
+            pairs_of_e = staged[:].rearrange("v b p e -> v (b p e)").bitcast(F32)
+            for blk in range(2):
+                nc.tensor.transpose(mean_words[half][:, blk, u, :], pairs_of_e[:, blk * P : (blk + 1) * P], ident[:])
+
+        def mean_out(half):
+            z_mean = sb.tile([P, HALF * PACK], BF16, name="z_mean%d" % half, align_bytes=64)
+            nc.scalar.copy(
+                out=z_mean[:].bitcast(F32).rearrange("p (b v u) -> p b v u", b=2, u=2),
+                in_=mean_words[half][:].rearrange("p b u v -> p b v u"),
+            )
+            return z_mean
+
+        w2_grp = sb.tile([P, N, PACK], BF16, name="w2_grp", align_bytes=64)
+        w34_grp = sb.tile([P, 2, N, PACK], BF16, name="w34_grp", align_bytes=64)
+        interleave(w2_grp[:], wz_raw[0][:])
+        interleave(w34_grp[:, 0], wz_raw[1][:])
 
         early = [sb.tile([P, PACK, HALF], F32, name="early%d" % d) for d in range(2)]
-        excess = sb.tile([P, PACK, HALF], F32, name="excess")
-        for u in range(2):
+        excess = shared.tile([P, PACK, HALF], F32, name="excess", offset=W3_RAW_AT)
+        for u, at in enumerate((DIFF_FIRST_AT, DIFF_LAST_AT)):
             for t in (2 * u, 2 * u + 1):
                 for d in range(2):
-                    gather(d, early[d], t, HALF)
-            diff = sb.tile([P, 2, HALF], F32, name="diff%d" % u)
+                    gather(d, early[d][:, t, :], t, 1)
+            diff = shared.tile([P, 2, HALF], F32, name="diff%d" % u, offset=at)
             nc.gpsimd.tensor_tensor(diff[:], early[1][:, 2 * u : 2 * u + 2], early[0][:, 2 * u : 2 * u + 2], SUB)
             nc.scalar.activation(excess[:, 2 * u : 2 * u + 2], diff[:], RELU)
-        ends = []
-        for n_op in range(2):
-            gb = sb.tile([P, HALF, PACK], BF16, name="end%d" % n_op, align_bytes=64)
-            nc.gpsimd.tensor_tensor(
-                gb[:].rearrange("p (c i) t -> p c t i", i=LINE),
-                early[n_op][:].rearrange("p t (c i) -> p c t i", i=LINE),
-                excess[:].rearrange("p t (c i) -> p c t i", i=LINE),
-                (ADD, SUB)[n_op],
-            )
-            ends.append(gb[:].rearrange("p v t -> p (v t)"))
-        larger, smaller = ends
-        first = rounded(gather_late(0, 0, 0), 0, HALF, "first")
-        second = rounded(gather_late(1, 0, 1), 0, HALF, "second")
-        g_third = gather_late(2, 0, 2)
+        interleave(w34_grp[:, 1], wz_raw[2][:])
+        wz_scales = sb.tile([P, 3, N], U8, name="wz_scales", align_bytes=64)
+        w2_codes = sb.tile([P, N], U32, name="w2_codes", align_bytes=64)
+        nc.vector.quantize_mx(out=w2_codes[:].bitcast(FP8X4), scales=wz_scales[:, 0], in_=flat(w2_grp[:]))
+        pair = [sb.tile([P, 2, HALF, PACK], BF16, name="pair%d" % half, align_bytes=64) for half in range(2)]
+        for d, op in enumerate((ADD, SUB)):
+            nc.gpsimd.tensor_tensor(woven(pair[1][:, d]), lines(early[d][:]), lines(excess[:]), op)
+
+        rounded_two = shared.tile([P, 2, HALF, PACK], BF16, name="rounded_two", offset=PAIR_ROUNDED_AT, align_bytes=64)
+        for d in range(2):
+            interleave(rounded_two[:, d], gather_list(d, 0, PAIR_LISTS_AT + d * GATHERED)[:])
+
+        g_third = gather_list(2, 0, THIRD_LIST_AT)
         mean_turn(0, 0)
-        third = {0: round_third(g_third, 0, HALF, "third0", held + 64 - 2048)}
+        third = {0: round_third(g_third, 0, HALF, "third_first", THIRD_FIRST_AT)}
         mean_turn(1, 0)
-        g_last = gather_late(2, HALF, 3)
+        g_last = gather_list(2, 1, THIRD_LIST_AT + GATHERED)
         for u in range(2):
             mean_turn(u, 1)
-        z_mean = [mean_out(0)]
-        third[HALF] = round_third(g_last, 0, P, "third1", stage[1][0] - 512)
-        z_mean.append(mean_out(1))
-        third[T - P] = round_third(g_last, P, HALF, "third2", stage[1][1] - 480)
+        z_means = [mean_out(0)]
+        third[HALF] = round_third(g_last, 0, P, "third_middle", THIRD_MIDDLE_AT)
+        z_means.append(mean_out(1))
+        third[T - P] = round_third(g_last, P, HALF, "third_last", THIRD_LAST_AT)
 
-        wz_codes = sb.tile([P, 3, N], U32, name="wz_codes", align_bytes=64)
-        wz_scales = sb.tile([P, 3, N], U8, name="wz_scales", align_bytes=64)
-        for s0, s1 in ((0, 2), (2, 3)):
-            nc.vector.quantize_mx(
-                out=wz_codes[:, s0:s1].rearrange("p s c -> p (s c)").bitcast(FP8X4),
-                scales=wz_scales[:, s0:s1].rearrange("p s c -> p (s c)"),
-                in_=wz_grp[:, s0:s1].rearrange("p s c j -> p (s c j)"),
-            )
+        w34_codes = shared.tile([P, 2, N], U32, name="w34_codes", offset=W34_CODES_AT, align_bytes=64)
+        nc.vector.quantize_mx(
+            out=w34_codes[:].rearrange("p s c -> p (s c)").bitcast(FP8X4),
+            scales=wz_scales[:, 1:].rearrange("p s c -> p (s c)"),
+            in_=w34_grp[:].rearrange("p s c j -> p (s c j)"),
+        )
+        wz_codes = [w2_codes[:], w34_codes[:, 0], w34_codes[:, 1]]
 
-        pair = sb.tile([P, 2, HALF * PACK], BF16, name="pair")
-        for n_op in range(2):
-            nc.vector.tensor_tensor(pair[:, n_op], first, second, (MAX, MIN)[n_op])
-        pairs = [(pair[:, 0], pair[:, 1]), (larger, smaller)]
+        for d, op in enumerate((MAX, MIN)):
+            nc.vector.tensor_tensor(flat(pair[0][:, d]), flat(rounded_two[:, 0]), flat(rounded_two[:, 1]), op)
 
-        z_codes = late.tile([P, 3, T], U32, name="z_codes", offset=held + 3712, align_bytes=64)
+        z_codes = shared.tile([P, 3, T], U32, name="z_codes", offset=Z_CODES_AT, align_bytes=64)
         z_scales = sb.tile([P, 3, T], U8, name="z_scales", align_bytes=64)
+        mean, largest, smallest = range(3)
 
         def quantise(s, a, b, z):
             nc.vector.quantize_mx(out=z_codes[:, s, a:b].bitcast(FP8X4), scales=z_scales[:, s, a:b], in_=z)
@@ -245,7 +252,7 @@ def tile_picked_wpna_none_l_kernel(
             for mt in range(2):
                 nc.tensor.matmul_mx(
                     out=accs[mt][:],
-                    lhsT=wz_codes[:, s, mt * P : (mt + 1) * P].bitcast(FP8X4),
+                    lhsT=wz_codes[s][:, mt * P : (mt + 1) * P].bitcast(FP8X4),
                     lhsT_scale=wz_scales[:, s, mt * P : (mt + 1) * P],
                     rhs=z_codes[:, s, a:b].bitcast(FP8X4),
                     rhs_scale=z_scales[:, s, a:b],
@@ -256,27 +263,27 @@ def tile_picked_wpna_none_l_kernel(
         out_rows = out.rearrange("(mt p) v -> p mt v", p=P)
         for n_piece, (a, b) in enumerate(((0, HALF), (HALF, T - P), (T - P, T))):
             last = b == T
-            order = (0, 1, 2) if last else (1, 2, 0)
+            order = (mean, largest, smallest) if last else (largest, smallest, mean)
             accs = [bank(2 + 2 * n_piece + mt, [P, b - a], "o_acc%d_%d" % (a, mt)) for mt in range(2)]
-            cols = slice(a % HALF * PACK, a % HALF * PACK + (b - a) * PACK)
+            two = pair[a // HALF][:, :, a % HALF : a % HALF + b - a]
             z_max = sb.tile([P, (b - a) * PACK], BF16, name="z_max%d" % a, align_bytes=64)
             z_min = sb.tile([P, (b - a) * PACK], BF16, name="z_min%d" % a, align_bytes=64)
-            nc.vector.tensor_tensor(z_max[:], pairs[a // HALF][0][:, cols], third[a], MAX)
-            nc.vector.tensor_tensor(z_min[:], pairs[a // HALF][1][:, cols], third[a], MIN)
+            nc.vector.tensor_tensor(z_max[:], flat(two[:, 0]), third[a], MAX)
+            nc.vector.tensor_tensor(z_min[:], flat(two[:, 1]), third[a], MIN)
             if last:
-                products(accs, 0, a, b, order)
-            for s, z in ((1, z_max), (2, z_min)):
+                products(accs, mean, a, b, order)
+            for s, z in ((largest, z_max), (smallest, z_min)):
                 quantise(s, a, b, z[:])
                 products(accs, s, a, b, order)
             if not last:
-                quantise(0, a, a + HALF, z_mean[n_piece][:])
-                products(accs, 0, a, b, order)
+                quantise(mean, a, a + HALF, z_means[n_piece][:])
+                products(accs, mean, a, b, order)
             res = sb.tile([P, 2, b - a], F32, name="res%d" % a, align_bytes=64)
-            for mt in range(2):
-                if last:
+            if last:
+                for mt in range(2):
                     nc.vector.tensor_copy(out=res[:, mt, :], in_=accs[mt][:])
                     nc.sync.dma_start(out=out_rows[:, mt, a:b], in_=res[:, mt, :])
-                else:
+            else:
+                for mt in range(2):
                     nc.scalar.copy(out=res[:, mt, :], in_=accs[mt][:])
-            if not last:
                 nc.sync.dma_start(out=out_rows[:, :, a:b], in_=res[:])

@@ -263,7 +263,7 @@ def tile_picked_wpna_none_l_kernel(
         out_rows = out.rearrange("(mt p) v -> p mt v", p=P)
         for n_piece, (a, b) in enumerate(((0, HALF), (HALF, T - P), (T - P, T))):
             last = b == T
-            order = (mean, largest, smallest) if last else (largest, smallest, mean)
+            order = ((largest, smallest, mean), (largest, mean, smallest), (mean, largest, smallest))[n_piece]
             accs = [bank(2 + 2 * n_piece + mt, [P, b - a], "o_acc%d_%d" % (a, mt)) for mt in range(2)]
             two = pair[a // HALF][:, :, a % HALF : a % HALF + b - a]
             z_max = sb.tile([P, (b - a) * PACK], BF16, name="z_max%d" % a, align_bytes=64)
@@ -272,16 +272,20 @@ def tile_picked_wpna_none_l_kernel(
             nc.vector.tensor_tensor(z_min[:], flat(two[:, 1]), third[a], MIN)
             if last:
                 products(accs, mean, a, b, order)
-            for s, z in ((largest, z_max), (smallest, z_min)):
-                quantise(s, a, b, z[:])
-                products(accs, s, a, b, order)
-            if not last:
+            quantise(largest, a, b, z_max[:])
+            products(accs, largest, a, b, order)
+            if n_piece == 1:
+                quantise(mean, a, a + HALF, z_means[n_piece][:])
+                products(accs, mean, a, b, order)
+            quantise(smallest, a, b, z_min[:])
+            products(accs, smallest, a, b, order)
+            if n_piece == 0:
                 quantise(mean, a, a + HALF, z_means[n_piece][:])
                 products(accs, mean, a, b, order)
             res = sb.tile([P, 2, b - a], F32, name="res%d" % a, align_bytes=64)
             if last:
                 for mt in range(2):
-                    nc.vector.tensor_copy(out=res[:, mt, :], in_=accs[mt][:])
+                    (nc.scalar.copy, nc.vector.tensor_copy)[mt](out=res[:, mt, :], in_=accs[mt][:])
                     nc.sync.dma_start(out=out_rows[:, mt, a:b], in_=res[:, mt, :])
             else:
                 for mt in range(2):

@@ -15,35 +15,14 @@ U8 = mybir.dt.uint8
 FP8X4 = mybir.dt.float8_e4m3fn_x4
 FP4X4 = mybir.dt.float4_e2m1fn_x4
 COPY = mybir.ActivationFunctionType.Copy
-RELU = mybir.ActivationFunctionType.Relu
 MAX = mybir.AluOpType.max
 MIN = mybir.AluOpType.min
-ADD = mybir.AluOpType.add
-SUB = mybir.AluOpType.subtract
 
 P = 128
 PACK = 4
 LINE = 4
 RUN = 8
 HALF = T // 2
-
-KIB = 1024
-GATHERED = 4 * KIB
-THIRD_FIRST_AT = 64
-STAGED_AT = THIRD_FIRST_AT + 2 * KIB
-THIRD_MIDDLE_AT = STAGED_AT + 2 * KIB - 512
-THIRD_LAST_AT = STAGED_AT + 3 * KIB - 480
-Z_CODES_AT = STAGED_AT + 3 * KIB + 576
-PAIR_LISTS_AT = 12 * KIB
-W2_RAW_AT = PAIR_LISTS_AT + GATHERED // 2
-THIRD_LIST_AT = PAIR_LISTS_AT + 2 * GATHERED
-DIFF_FIRST_AT = THIRD_LIST_AT + GATHERED - KIB
-W3_RAW_AT = 32 * KIB
-W4_RAW_AT = 36 * KIB
-PAIR_ROUNDED_AT = 44 * KIB
-DIFF_LAST_AT = PAIR_ROUNDED_AT - KIB
-PLANE_AT = (56 * KIB, 58 * KIB, 50 * KIB, 48 * KIB)
-W34_CODES_AT = PLANE_AT[2]
 
 
 def tile_picked_wpna_none_l_kernel(
@@ -67,8 +46,13 @@ def tile_picked_wpna_none_l_kernel(
         def flat(words):
             return words.rearrange("p v t -> p (v t)")
 
-        def interleave(dst, src):
-            nc.scalar.copy(out=woven(dst), in_=lines(src))
+        def interleave(copy, dst, src):
+            copy(out=woven(dst), in_=lines(src))
+
+        def interleave_many(dst, src):
+            nc.vector.tensor_copy(
+                out=dst.rearrange("p s (c i) t -> p s c t i", i=LINE), in_=src.rearrange("p s t (c i) -> p s c t i", i=LINE)
+            )
 
         w1_rows = w1.rearrange("(p s j) c -> s p j c", s=2, j=2)
         w1_raw = [sb.tile([P, 2, H], F32, name="w1_raw%d" % s) for s in range(2)]
@@ -85,18 +69,16 @@ def tile_picked_wpna_none_l_kernel(
         lists = [sb.tile([P, T // 16], U16, name="pos%d" % d) for d in range(3)]
         for tile, pos in zip(lists, (pos1, pos2, pos3)):
             nc.sync.dma_start(tile[:], pos)
-        wz_raw = []
-        for s, (w, at) in enumerate(((w2, W2_RAW_AT), (w3, W3_RAW_AT), (w4, W4_RAW_AT))):
-            raw = shared.tile([P, PACK, N], F32, name="wz_raw%d" % s, offset=at)
+        wz_raw = sb.tile([P, 3, PACK, N], F32, name="wz_raw")
+        for s, w in enumerate((w2, w3, w4)):
             rows = w.rearrange("(g u r e) c -> u g r (e c)", u=2, r=RUN, e=2)
             for u in range(2):
-                nc.sync.dma_start(out=raw[:, 2 * u : 2 * u + 2, :].rearrange("p e c -> p (e c)"), in_=rows[u])
-            wz_raw.append(raw)
+                nc.sync.dma_start(out=wz_raw[:, s, 2 * u : 2 * u + 2, :].rearrange("p e c -> p (e c)"), in_=rows[u])
 
         ident = sb.tile([P, P], F32, name="ident")
         make_identity(nc, ident[:])
 
-        h = [shared.tile([P, T], F32, name="h%d" % t, offset=PLANE_AT[t]) for t in range(PACK)]
+        h = [sb.tile([P, T], F32, name="h%d" % t) for t in range(PACK)]
         w1_grp = sb.tile([P, PACK, P, PACK], BF16, name="w1_grp", align_bytes=64)
         w1_from = [
             raw[:].rearrange("p j (g u a i e) -> p u e g a j i", u=2, a=RUN // LINE, i=LINE, e=2) for raw in w1_raw
@@ -148,146 +130,177 @@ def tile_picked_wpna_none_l_kernel(
             w1_quantise(t, 0, P)
             project(t, 0, T, n_bank, nc.scalar.copy)
 
-        sums = [[bank(4 + 2 * u + half, [P, 2, 2, P], "sum%d_%d" % (u, half)) for half in range(2)] for u in range(2)]
+        gathered = [sb.tile([P, 2, PACK, HALF], F32, name="gathered%d" % half) for half in range(2)]
+        pieces = ((0, HALF), (HALF, T - P), (T - P, T))
+        thirds = {}
 
-        def gather(d, dst, t, half):
-            nc.vector.tensor_copy(dst, h[t][:].indirect(lists[d][:, half * HALF // 16 : (half + 1) * HALF // 16]))
-            for blk in range(2):
+        def on_vector(dst, src):
+            nc.vector.tensor_copy(dst, src)
+
+        def on_scalar(dst, src):
+            nc.scalar.activation(dst, src, COPY)
+
+        def columns(d, a, b):
+            if d == 2:
+                first = max(x for x in thirds if x <= a)
+                return thirds[first][:, :, a - first : b - first]
+            return gathered[a // HALF][:, d, :, a % HALF : a % HALF + b - a]
+
+        sums = [bank(4 + blk, [P, PACK, P], "sum%d" % blk) for blk in range(T // P)]
+        added = [0] * len(sums)
+
+        def gather(fetch, d, t, a, b):
+            fetch(columns(d, a, b)[:, t], h[t][:].indirect(lists[d][:, a // 16 : b // 16]))
+            for blk in range(a // P, b // P):
                 nc.tensor.matmul(
-                    sums[t // 2][half][:, blk, t % 2, :],
-                    lhsT=dst[:, blk * P : (blk + 1) * P],
+                    sums[blk][:, t, :],
+                    lhsT=columns(d, blk * P, (blk + 1) * P)[:, t],
                     rhs=ident[:],
                     is_transpose=True,
-                    start=(d == 0 and t % 2 == 0 and blk == 0),
-                    stop=(d == 2 and t % 2 == 1 and blk == 1),
+                    start=added[blk] == 0,
+                    stop=added[blk] == 3 * PACK - 1,
+                )
+                added[blk] = added[blk] + 1
+
+        for half, fetch in enumerate((on_vector, on_scalar)):
+            for t in range(PACK):
+                for d in range(2):
+                    gather(on_vector if (d, t) == (0, 3) else fetch, d, t, half * HALF, (half + 1) * HALF)
+
+        wz_grp = sb.tile([P, 3, N, PACK], BF16, name="wz_grp", align_bytes=64)
+        wz_codes = sb.tile([P, 3, N], U32, name="wz_codes", align_bytes=64)
+        wz_scales = sb.tile([P, 3, N], U8, name="wz_scales", align_bytes=64)
+        interleave(nc.vector.tensor_copy, wz_grp[:, 0], wz_raw[:, 0])
+        interleave_many(wz_grp[:, 1:], wz_raw[:, 1:])
+        for s0, s1 in ((0, 1), (1, 3)):
+            nc.vector.quantize_mx(
+                out=wz_codes[:, s0:s1].rearrange("p s c -> p (s c)").bitcast(FP8X4),
+                scales=wz_scales[:, s0:s1].rearrange("p s c -> p (s c)"),
+                in_=wz_grp[:, s0:s1].rearrange("p s c j -> p (s c j)"),
+            )
+
+        z_codes = {a: sb.tile([P, 3, b - a], U32, name="z_codes%d" % a, align_bytes=64) for a, b in pieces}
+        z_scales = {a: sb.tile([P, 3, b - a], U8, name="z_scales%d" % a, align_bytes=64) for a, b in pieces}
+        mean, largest, smallest = range(3)
+
+        def quantise(s0, s1, a, z):
+            nc.vector.quantize_mx(
+                out=z_codes[a][:, s0:s1].rearrange("p s v -> p (s v)").bitcast(FP8X4),
+                scales=z_scales[a][:, s0:s1].rearrange("p s v -> p (s v)"),
+                in_=z,
+            )
+
+        def products(accs, s, a, start, stop):
+            for mt in range(2):
+                nc.tensor.matmul_mx(
+                    out=accs[mt],
+                    lhsT=wz_codes[:, s, mt * P : (mt + 1) * P].bitcast(FP8X4),
+                    lhsT_scale=wz_scales[:, s, mt * P : (mt + 1) * P],
+                    rhs=z_codes[a][:, s].bitcast(FP8X4),
+                    rhs_scale=z_scales[a][:, s],
+                    start=start and (mt == 0 or a == T - P),
+                    stop=stop and (mt == 1 or a == T - P),
                 )
 
-        def gather_list(d, half, at):
-            g = shared.tile([P, PACK, HALF], F32, name="g%d_%d" % (d, half), offset=at)
-            for t in range(PACK):
-                gather(d, g[:, t, :], t, half)
-            return g
+        def rounded(copy, a, b):
+            r = sb.tile([P, b - a, PACK], BF16, name="third%d" % a, align_bytes=64)
+            interleave(copy, r[:], columns(2, a, b))
+            return r
 
-        mean_words = [bank(half, [P, 2, 2, P], "mean_words%d" % half) for half in range(2)]
+        def extremes(a, b, hi, lo, name):
+            z = sb.tile([P, 2, b - a, PACK], BF16, name="%s%d" % (name, a), align_bytes=64)
+            nc.vector.tensor_tensor(flat(z[:, 0]), flat(hi[0]), flat(hi[1]), MAX)
+            nc.vector.tensor_tensor(flat(z[:, 1]), flat(lo[0]), flat(lo[1]), MIN)
+            return z
 
-        def round_third(g, a, b, name, at):
-            rounded = shared.tile([P, b - a, PACK], BF16, name=name, offset=at)
-            interleave(rounded[:], g[:, :, a:b])
-            return flat(rounded[:])
+        pair = []
+        for half in range(2):
+            two = sb.tile([P, 2, HALF, PACK], BF16, name="two%d" % half, align_bytes=64)
+            interleave_many(two[:], gathered[half][:])
+            lists12 = (two[:, 0], two[:, 1])
+            pair.append(extremes(half * HALF, (half + 1) * HALF, lists12, lists12, "pair"))
 
-        def mean_turn(u, half):
-            staged = shared.tile(
-                [P, 2, P, 2], BF16, name="staged%d_%d" % (u, half), offset=STAGED_AT + KIB * (2 * u + half)
+        words = {a: bank(n, [P, (b - a) // P, 2, P], "words%d" % a) for n, (a, b) in enumerate(pieces)}
+
+        def turn(a, blk):
+            staged = shared.tile([P, 2, P, 2], BF16, name="staged%d" % blk, offset=4096 * blk)
+            nc.scalar.activation(
+                staged[:], sums[blk][:].rearrange("v (u e) p -> v u p e", e=2), COPY, scale=1.0 / 3.0
             )
-            nc.scalar.activation(staged[:], sums[u][half][:].rearrange("v b e p -> v b p e"), COPY, scale=1.0 / 3.0)
-            pairs_of_e = staged[:].rearrange("v b p e -> v (b p e)").bitcast(F32)
-            for blk in range(2):
-                nc.tensor.transpose(mean_words[half][:, blk, u, :], pairs_of_e[:, blk * P : (blk + 1) * P], ident[:])
+            pairs = staged[:].rearrange("v u p e -> v (u p e)").bitcast(F32)
+            for u in range(2):
+                nc.tensor.transpose(words[a][:, blk - a // P, u, :], pairs[:, u * P : (u + 1) * P], ident[:])
 
-        def mean_out(half):
-            z_mean = sb.tile([P, HALF * PACK], BF16, name="z_mean%d" % half, align_bytes=64)
+        def mean_out(a, b):
+            z_mean = sb.tile([P, (b - a) * PACK], BF16, name="z_mean%d" % a, align_bytes=64)
             nc.scalar.copy(
-                out=z_mean[:].bitcast(F32).rearrange("p (b v u) -> p b v u", b=2, u=2),
-                in_=mean_words[half][:].rearrange("p b u v -> p b v u"),
+                out=z_mean[:].bitcast(F32).rearrange("p (b v u) -> p b v u", v=P, u=2),
+                in_=words[a][:].rearrange("p b u v -> p b v u"),
             )
             return z_mean
 
-        w2_grp = sb.tile([P, N, PACK], BF16, name="w2_grp", align_bytes=64)
-        w34_grp = sb.tile([P, 2, N, PACK], BF16, name="w34_grp", align_bytes=64)
-        interleave(w2_grp[:], wz_raw[0][:])
-        interleave(w34_grp[:, 0], wz_raw[1][:])
-
-        early = [sb.tile([P, PACK, HALF], F32, name="early%d" % d) for d in range(2)]
-        excess = shared.tile([P, PACK, HALF], F32, name="excess", offset=W3_RAW_AT)
-        for u, at in enumerate((DIFF_FIRST_AT, DIFF_LAST_AT)):
-            for t in (2 * u, 2 * u + 1):
-                for d in range(2):
-                    gather(d, early[d][:, t, :], t, 1)
-            diff = shared.tile([P, 2, HALF], F32, name="diff%d" % u, offset=at)
-            nc.gpsimd.tensor_tensor(diff[:], early[1][:, 2 * u : 2 * u + 2], early[0][:, 2 * u : 2 * u + 2], SUB)
-            nc.scalar.activation(excess[:, 2 * u : 2 * u + 2], diff[:], RELU)
-        interleave(w34_grp[:, 1], wz_raw[2][:])
-        wz_scales = sb.tile([P, 3, N], U8, name="wz_scales", align_bytes=64)
-        w2_codes = sb.tile([P, N], U32, name="w2_codes", align_bytes=64)
-        nc.vector.quantize_mx(out=w2_codes[:].bitcast(FP8X4), scales=wz_scales[:, 0], in_=flat(w2_grp[:]))
-        pair = [sb.tile([P, 2, HALF, PACK], BF16, name="pair%d" % half, align_bytes=64) for half in range(2)]
-        for d, op in enumerate((ADD, SUB)):
-            nc.gpsimd.tensor_tensor(woven(pair[1][:, d]), lines(early[d][:]), lines(excess[:]), op)
-
-        rounded_two = shared.tile([P, 2, HALF, PACK], BF16, name="rounded_two", offset=PAIR_ROUNDED_AT, align_bytes=64)
-        for d in range(2):
-            interleave(rounded_two[:, d], gather_list(d, 0, PAIR_LISTS_AT + d * GATHERED)[:])
-
-        g_third = gather_list(2, 0, THIRD_LIST_AT)
-        mean_turn(0, 0)
-        third = {0: round_third(g_third, 0, HALF, "third_first", THIRD_FIRST_AT)}
-        mean_turn(1, 0)
-        g_last = gather_list(2, 1, THIRD_LIST_AT + GATHERED)
-        for u in range(2):
-            mean_turn(u, 1)
-        z_means = [mean_out(0)]
-        third[HALF] = round_third(g_last, 0, P, "third_middle", THIRD_MIDDLE_AT)
-        z_means.append(mean_out(1))
-        third[T - P] = round_third(g_last, P, HALF, "third_last", THIRD_LAST_AT)
-
-        w34_codes = shared.tile([P, 2, N], U32, name="w34_codes", offset=W34_CODES_AT, align_bytes=64)
-        nc.vector.quantize_mx(
-            out=w34_codes[:].rearrange("p s c -> p (s c)").bitcast(FP8X4),
-            scales=wz_scales[:, 1:].rearrange("p s c -> p (s c)"),
-            in_=w34_grp[:].rearrange("p s c j -> p (s c j)"),
-        )
-        wz_codes = [w2_codes[:], w34_codes[:, 0], w34_codes[:, 1]]
-
-        for d, op in enumerate((MAX, MIN)):
-            nc.vector.tensor_tensor(flat(pair[0][:, d]), flat(rounded_two[:, 0]), flat(rounded_two[:, 1]), op)
-
-        z_codes = shared.tile([P, 3, T], U32, name="z_codes", offset=Z_CODES_AT, align_bytes=64)
-        z_scales = sb.tile([P, 3, T], U8, name="z_scales", align_bytes=64)
-        mean, largest, smallest = range(3)
-
-        def quantise(s, a, b, z):
-            nc.vector.quantize_mx(out=z_codes[:, s, a:b].bitcast(FP8X4), scales=z_scales[:, s, a:b], in_=z)
-
-        def products(accs, s, a, b, order):
-            for mt in range(2):
-                nc.tensor.matmul_mx(
-                    out=accs[mt][:],
-                    lhsT=wz_codes[s][:, mt * P : (mt + 1) * P].bitcast(FP8X4),
-                    lhsT_scale=wz_scales[:, s, mt * P : (mt + 1) * P],
-                    rhs=z_codes[:, s, a:b].bitcast(FP8X4),
-                    rhs_scale=z_scales[:, s, a:b],
-                    start=(s == order[0]),
-                    stop=(s == order[-1]),
-                )
+        for a, b in pieces[:2]:
+            thirds[a] = sb.tile([P, PACK, b - a], F32, name="gathered_third%d" % a)
+            for t in range(PACK):
+                gather(on_scalar, 2, t, a, b)
+        turn(0, 0)
+        turn(0, 1)
+        means = {0: mean_out(0, HALF)}
+        thirds[T - P] = shared.tile([P, PACK, P], F32, name="gathered_last", offset=0)
+        for t in range(PACK):
+            gather(on_scalar, 2, t, T - P, T)
+        turn(HALF, 2)
+        turn(T - P, 3)
+        third_last = rounded(nc.scalar.copy, T - P, T)
+        means[HALF] = mean_out(HALF, T - P)
+        means[T - P] = mean_out(T - P, T)
 
         out_rows = out.rearrange("(mt p) v -> p mt v", p=P)
-        for n_piece, (a, b) in enumerate(((0, HALF), (HALF, T - P), (T - P, T))):
-            last = b == T
-            order = ((largest, smallest, mean), (largest, mean, smallest), (mean, largest, smallest))[n_piece]
-            accs = [bank(2 + 2 * n_piece + mt, [P, b - a], "o_acc%d_%d" % (a, mt)) for mt in range(2)]
-            two = pair[a // HALF][:, :, a % HALF : a % HALF + b - a]
-            z_max = sb.tile([P, (b - a) * PACK], BF16, name="z_max%d" % a, align_bytes=64)
-            z_min = sb.tile([P, (b - a) * PACK], BF16, name="z_min%d" % a, align_bytes=64)
-            nc.vector.tensor_tensor(z_max[:], flat(two[:, 0]), third[a], MAX)
-            nc.vector.tensor_tensor(z_min[:], flat(two[:, 1]), third[a], MIN)
-            if last:
-                products(accs, mean, a, b, order)
-            quantise(largest, a, b, z_max[:])
-            products(accs, largest, a, b, order)
-            if n_piece == 1:
-                quantise(mean, a, a + HALF, z_means[n_piece][:])
-                products(accs, mean, a, b, order)
-            quantise(smallest, a, b, z_min[:])
-            products(accs, smallest, a, b, order)
-            if n_piece == 0:
-                quantise(mean, a, a + HALF, z_means[n_piece][:])
-                products(accs, mean, a, b, order)
+        third = [rounded(nc.vector.tensor_copy, a, b) for a, b in pieces[:2]] + [third_last]
+        z = [sb.tile([P, 2, b - a, PACK], BF16, name="z%d" % a, align_bytes=64) for a, b in pieces]
+        joint = [bank(7, [P, 2, HALF], "o_first"), bank(6, [P, 2, P], "o_middle")]
+        accs = [[acc[:, mt] for mt in range(2)] for acc in joint]
+        accs.append([bank(4 + mt, [P, P], "o_last%d" % mt)[:] for mt in range(2)])
+
+        def extreme(n, side):
+            a, b = pieces[n]
+            two = pair[a // HALF][:, side, a % HALF : a % HALF + b - a]
+            nc.vector.tensor_tensor(flat(z[n][:, side]), flat(two), flat(third[n][:]), (MAX, MIN)[side])
+
+        def extremes_in(n, start):
+            a = pieces[n][0]
+            quantise(largest, 3, a, z[n][:].rearrange("p s v t -> p (s v t)"))
+            products(accs[n], largest, a, start, False)
+            products(accs[n], smallest, a, False, not start)
+
+        def mean_in(n, start):
+            a = pieces[n][0]
+            quantise(mean, largest, a, means[a][:])
+            products(accs[n], mean, a, start, not start)
+
+        def leave(n):
+            a, b = pieces[n]
             res = sb.tile([P, 2, b - a], F32, name="res%d" % a, align_bytes=64)
-            if last:
+            if b == T:
                 for mt in range(2):
-                    (nc.scalar.copy, nc.vector.tensor_copy)[mt](out=res[:, mt, :], in_=accs[mt][:])
+                    (nc.scalar.copy, nc.vector.tensor_copy)[mt](out=res[:, mt, :], in_=accs[n][mt])
                     nc.sync.dma_start(out=out_rows[:, mt, a:b], in_=res[:, mt, :])
             else:
-                for mt in range(2):
-                    nc.scalar.copy(out=res[:, mt, :], in_=accs[mt][:])
+                nc.scalar.copy(out=res[:], in_=joint[n][:])
                 nc.sync.dma_start(out=out_rows[:, :, a:b], in_=res[:])
+
+        extreme(0, 0)
+        extreme(0, 1)
+        extreme(1, 0)
+        extremes_in(0, True)
+        extreme(1, 1)
+        mean_in(0, False)
+        leave(0)
+        extreme(2, 0)
+        extremes_in(1, True)
+        extreme(2, 1)
+        mean_in(1, False)
+        leave(1)
+        mean_in(2, True)
+        extremes_in(2, False)
+        leave(2)

@@ -17,6 +17,8 @@ FP4X4 = mybir.dt.float4_e2m1fn_x4
 COPY = mybir.ActivationFunctionType.Copy
 MAX = mybir.AluOpType.max
 MIN = mybir.AluOpType.min
+MULT = mybir.AluOpType.mult
+ADD = mybir.AluOpType.add
 
 P = 128
 PACK = 4
@@ -67,19 +69,24 @@ def tile_picked_wpna_none_l_kernel(
                 out=xs[32 * q : 32 * q + 4, :].bitcast(I32), in_=x_scales[0, 4 * q : 4 * q + 4, :].bitcast(I32)
             )
         lists = [sb.tile([P, T // 16], U16, name="pos%d" % d) for d in range(3)]
-        for tile, pos in zip(lists, (pos1, pos2, pos3)):
+        for tile, pos in zip(lists[:2], (pos1, pos2)):
             nc.sync.dma_start(tile[:], pos)
-        wz_raw = sb.tile([P, 3, PACK, N], F32, name="wz_raw")
-        for s, w in enumerate((w2, w3, w4)):
+        wz_raw = [sb.tile([P, PACK, N], F32, name="wz_raw%d" % s) for s in range(3)]
+        for raw, w in zip(wz_raw, (w2, w3, w4)):
             rows = w.rearrange("(g u r e) c -> u g r (e c)", u=2, r=RUN, e=2)
             for u in range(2):
-                nc.sync.dma_start(out=wz_raw[:, s, 2 * u : 2 * u + 2, :].rearrange("p e c -> p (e c)"), in_=rows[u])
+                nc.sync.dma_start(out=raw[:, 2 * u : 2 * u + 2, :].rearrange("p e c -> p (e c)"), in_=rows[u])
+            if raw is wz_raw[0]:
+                nc.sync.dma_start(lists[2][:], pos3)
+
 
         ident = sb.tile([P, P], F32, name="ident")
         make_identity(nc, ident[:])
 
-        h = [sb.tile([P, T], F32, name="h%d" % t) for t in range(PACK)]
-        w1_grp = sb.tile([P, PACK, P, PACK], BF16, name="w1_grp", align_bytes=64)
+        h_all = sb.tile([P, PACK * T], F32, name="h_all")
+        h = [h_all[:, (PACK - 1 - t) * T : (PACK - t) * T] for t in range(PACK)]
+        wide = [h_all[:, (PACK - 1 - t) * T : (PACK + 1 - t) * T] for t in range(1, PACK)]
+        w1_grp = shared.tile([P, PACK, P, PACK], BF16, name="w1_grp", align_bytes=64, offset=16384)
         w1_from = [
             raw[:].rearrange("p j (g u a i e) -> p u e g a j i", u=2, a=RUN // LINE, i=LINE, e=2) for raw in w1_raw
         ]
@@ -130,9 +137,9 @@ def tile_picked_wpna_none_l_kernel(
             w1_quantise(t, 0, P)
             project(t, 0, T, n_bank, nc.scalar.copy)
 
-        gathered = [sb.tile([P, 2, PACK, HALF], F32, name="gathered%d" % half) for half in range(2)]
+        lists12 = sb.tile([P, 2, PACK, T], F32, name="lists12")
         pieces = ((0, HALF), (HALF, T - P), (T - P, T))
-        thirds = {}
+        list3 = [sb.tile([P, PACK, HALF], F32, name="list3_first")]
 
         def on_vector(dst, src):
             nc.vector.tensor_copy(dst, src)
@@ -142,15 +149,15 @@ def tile_picked_wpna_none_l_kernel(
 
         def columns(d, a, b):
             if d == 2:
-                first = max(x for x in thirds if x <= a)
-                return thirds[first][:, :, a - first : b - first]
-            return gathered[a // HALF][:, d, :, a % HALF : a % HALF + b - a]
+                return list3[a // HALF][:, :, a % HALF : a % HALF + b - a]
+            return lists12[:, d, :, a:b]
 
         sums = [bank(4 + blk, [P, PACK, P], "sum%d" % blk) for blk in range(T // P)]
         added = [0] * len(sums)
 
         def gather(fetch, d, t, a, b):
-            fetch(columns(d, a, b)[:, t], h[t][:].indirect(lists[d][:, a // 16 : b // 16]))
+            window = wide[t - 1] if b - a == T else h[t]
+            fetch(columns(d, a, b)[:, t], window.indirect(lists[d][:, a // 16 : b // 16]))
             for blk in range(a // P, b // P):
                 nc.tensor.matmul(
                     sums[blk][:, t, :],
@@ -162,16 +169,25 @@ def tile_picked_wpna_none_l_kernel(
                 )
                 added[blk] = added[blk] + 1
 
-        for half, fetch in enumerate((on_vector, on_scalar)):
-            for t in range(PACK):
-                for d in range(2):
-                    gather(on_vector if (d, t) == (0, 3) else fetch, d, t, half * HALF, (half + 1) * HALF)
+        for a in (0, HALF):
+            for d in range(2):
+                gather(on_vector, d, 0, a, a + HALF)
+        for d in range(2):
+            gather(on_scalar, d, 2, 0, T)
+            gather(on_vector, d, 1, 0, T)
+        gather(on_scalar, 0, 3, 0, T)
+        for t in range(2):
+            gather(on_vector, 2, t, 0, HALF)
+        gather(on_scalar, 1, 3, 0, HALF)
+        for t in range(2, PACK):
+            gather(on_scalar, 2, t, 0, HALF)
+        gather(on_scalar, 1, 3, HALF, T)
 
-        wz_grp = sb.tile([P, 3, N, PACK], BF16, name="wz_grp", align_bytes=64)
+        wz_grp = shared.tile([P, 3, N, PACK], BF16, name="wz_grp", align_bytes=64, offset=16384)
         wz_codes = sb.tile([P, 3, N], U32, name="wz_codes", align_bytes=64)
         wz_scales = sb.tile([P, 3, N], U8, name="wz_scales", align_bytes=64)
-        interleave(nc.vector.tensor_copy, wz_grp[:, 0], wz_raw[:, 0])
-        interleave_many(wz_grp[:, 1:], wz_raw[:, 1:])
+        for s in range(3):
+            nc.gpsimd.tensor_scalar(wz_grp[:, s], wz_raw[s][:].rearrange("p t c -> p c t"), 1.0, 0.0, MULT, ADD)
         for s0, s1 in ((0, 1), (1, 3)):
             nc.vector.quantize_mx(
                 out=wz_codes[:, s0:s1].rearrange("p s c -> p (s c)").bitcast(FP8X4),
@@ -207,23 +223,21 @@ def tile_picked_wpna_none_l_kernel(
             interleave(copy, r[:], columns(2, a, b))
             return r
 
-        def extremes(a, b, hi, lo, name):
-            z = sb.tile([P, 2, b - a, PACK], BF16, name="%s%d" % (name, a), align_bytes=64)
-            nc.vector.tensor_tensor(flat(z[:, 0]), flat(hi[0]), flat(hi[1]), MAX)
-            nc.vector.tensor_tensor(flat(z[:, 1]), flat(lo[0]), flat(lo[1]), MIN)
-            return z
-
-        pair = []
-        for half in range(2):
+        def pair_of(half):
             two = sb.tile([P, 2, HALF, PACK], BF16, name="two%d" % half, align_bytes=64)
-            interleave_many(two[:], gathered[half][:])
-            lists12 = (two[:, 0], two[:, 1])
-            pair.append(extremes(half * HALF, (half + 1) * HALF, lists12, lists12, "pair"))
+            interleave_many(two[:], lists12[:, :, :, half * HALF : (half + 1) * HALF])
+            return two
+
+        def pair_extremes(two, half):
+            pair = sb.tile([P, 2, HALF, PACK], BF16, name="pair%d" % half, align_bytes=64)
+            for side, op in enumerate((MAX, MIN)):
+                nc.vector.tensor_tensor(flat(pair[:, side]), flat(two[:, 0]), flat(two[:, 1]), op)
+            return pair
 
         words = {a: bank(n, [P, (b - a) // P, 2, P], "words%d" % a) for n, (a, b) in enumerate(pieces)}
 
-        def turn(a, blk):
-            staged = shared.tile([P, 2, P, 2], BF16, name="staged%d" % blk, offset=4096 * blk)
+        def turn(a, blk, at):
+            staged = shared.tile([P, 2, P, 2], BF16, name="staged%d" % blk, offset=at)
             nc.scalar.activation(
                 staged[:], sums[blk][:].rearrange("v (u e) p -> v u p e", e=2), COPY, scale=1.0 / 3.0
             )
@@ -239,28 +253,13 @@ def tile_picked_wpna_none_l_kernel(
             )
             return z_mean
 
-        for a, b in pieces[:2]:
-            thirds[a] = sb.tile([P, PACK, b - a], F32, name="gathered_third%d" % a)
-            for t in range(PACK):
-                gather(on_scalar, 2, t, a, b)
-        turn(0, 0)
-        turn(0, 1)
-        means = {0: mean_out(0, HALF)}
-        thirds[T - P] = shared.tile([P, PACK, P], F32, name="gathered_last", offset=0)
-        for t in range(PACK):
-            gather(on_scalar, 2, t, T - P, T)
-        turn(HALF, 2)
-        turn(T - P, 3)
-        third_last = rounded(nc.scalar.copy, T - P, T)
-        means[HALF] = mean_out(HALF, T - P)
-        means[T - P] = mean_out(T - P, T)
-
         out_rows = out.rearrange("(mt p) v -> p mt v", p=P)
-        third = [rounded(nc.vector.tensor_copy, a, b) for a, b in pieces[:2]] + [third_last]
-        z = [sb.tile([P, 2, b - a, PACK], BF16, name="z%d" % a, align_bytes=64) for a, b in pieces]
-        joint = [bank(7, [P, 2, HALF], "o_first"), bank(6, [P, 2, P], "o_middle")]
+        z = [shared.tile([P, 2, HALF, PACK], BF16, name="z_first", align_bytes=64, offset=8192)]
+        z.extend(sb.tile([P, 2, P, PACK], BF16, name="z%d" % a, align_bytes=64) for a, b in pieces[1:])
+        joint = [bank(3, [P, 2, HALF], "o_first"), bank(4, [P, 2, P], "o_middle")]
         accs = [[acc[:, mt] for mt in range(2)] for acc in joint]
-        accs.append([bank(4 + mt, [P, P], "o_last%d" % mt)[:] for mt in range(2)])
+        accs.append([bank(5 * mt, [P, P], "o_last%d" % mt)[:] for mt in range(2)])
+        pair, third, means = {}, {}, {}
 
         def extreme(n, side):
             a, b = pieces[n]
@@ -275,7 +274,7 @@ def tile_picked_wpna_none_l_kernel(
 
         def mean_in(n, start):
             a = pieces[n][0]
-            quantise(mean, largest, a, means[a][:])
+            quantise(mean, largest, a, means[n][:])
             products(accs[n], mean, a, start, not start)
 
         def leave(n):
@@ -289,13 +288,33 @@ def tile_picked_wpna_none_l_kernel(
                 nc.scalar.copy(out=res[:], in_=joint[n][:])
                 nc.sync.dma_start(out=out_rows[:, :, a:b], in_=res[:])
 
+        turn(0, 0, 0)
+        turn(0, 1, 4096)
+        means[0] = mean_out(0, HALF)
+        list3.append(shared.tile([P, PACK, HALF], F32, name="list3_last", offset=0))
+        for t in range(PACK):
+            gather(on_scalar, 2, t, HALF, T)
+
+        two = pair_of(0)
+        third[0] = rounded(nc.vector.tensor_copy, 0, HALF)
+        pair[0] = pair_extremes(two, 0)
         extreme(0, 0)
         extreme(0, 1)
-        extreme(1, 0)
-        extremes_in(0, True)
-        extreme(1, 1)
-        mean_in(0, False)
+        mean_in(0, True)
+        extremes_in(0, False)
+
+        third[1] = rounded(nc.scalar.copy, HALF, T - P)
+        turn(HALF, 2, 8192)
+        third[2] = rounded(nc.scalar.copy, T - P, T)
+        turn(T - P, 3, 5120)
         leave(0)
+        means[1] = mean_out(HALF, T - P)
+        means[2] = mean_out(T - P, T)
+
+        two = pair_of(1)
+        pair[1] = pair_extremes(two, 1)
+        extreme(1, 0)
+        extreme(1, 1)
         extreme(2, 0)
         extremes_in(1, True)
         extreme(2, 1)

@@ -176,10 +176,9 @@ def tile_picked_wpna_none_l_kernel(
             gather(on_scalar, d, 2, 0, T)
             gather(on_vector, d, 1, 0, T)
         gather(on_scalar, 0, 3, 0, T)
-        for t in range(2):
-            gather(on_vector, 2, t, 0, HALF)
+        gather(on_vector, 2, 0, 0, HALF)
         gather(on_scalar, 1, 3, 0, HALF)
-        for t in range(2, PACK):
+        for t in range(1, PACK):
             gather(on_scalar, 2, t, 0, HALF)
         gather(on_scalar, 1, 3, HALF, T)
 
@@ -187,7 +186,7 @@ def tile_picked_wpna_none_l_kernel(
         wz_codes = sb.tile([P, 3, N], U32, name="wz_codes", align_bytes=64)
         wz_scales = sb.tile([P, 3, N], U8, name="wz_scales", align_bytes=64)
         for s in range(3):
-            nc.gpsimd.tensor_scalar(wz_grp[:, s], wz_raw[s][:].rearrange("p t c -> p c t"), 1.0, 0.0, MULT, ADD)
+            interleave(nc.vector.tensor_copy, wz_grp[:, s], wz_raw[s][:])
         for s0, s1 in ((0, 1), (1, 3)):
             nc.vector.quantize_mx(
                 out=wz_codes[:, s0:s1].rearrange("p s c -> p (s c)").bitcast(FP8X4),

@@ -176,18 +176,20 @@ def tile_picked_wpna_none_l_kernel(
             gather(on_scalar, d, 2, 0, T)
             gather(on_vector, d, 1, 0, T)
         gather(on_scalar, 0, 3, 0, T)
-        gather(on_vector, 2, 0, 0, HALF)
+        for t in range(2):
+            gather(on_vector, 2, t, 0, HALF)
         gather(on_scalar, 1, 3, 0, HALF)
-        for t in range(1, PACK):
+        for t in range(2, PACK):
             gather(on_scalar, 2, t, 0, HALF)
         gather(on_scalar, 1, 3, HALF, T)
 
         wz_grp = shared.tile([P, 3, N, PACK], BF16, name="wz_grp", align_bytes=64, offset=16384)
         wz_codes = sb.tile([P, 3, N], U32, name="wz_codes", align_bytes=64)
         wz_scales = sb.tile([P, 3, N], U8, name="wz_scales", align_bytes=64)
-        for s in range(3):
-            interleave(nc.vector.tensor_copy, wz_grp[:, s], wz_raw[s][:])
-        for s0, s1 in ((0, 1), (1, 3)):
+        for s in range(2):
+            nc.gpsimd.tensor_scalar(wz_grp[:, s], wz_raw[s][:].rearrange("p t c -> p c t"), 1.0, 0.0, MULT, ADD)
+        interleave(nc.vector.tensor_copy, wz_grp[:, 2], wz_raw[2][:])
+        for s0, s1 in ((0, 2), (2, 3)):
             nc.vector.quantize_mx(
                 out=wz_codes[:, s0:s1].rearrange("p s c -> p (s c)").bitcast(FP8X4),
                 scales=wz_scales[:, s0:s1].rearrange("p s c -> p (s c)"),
@@ -299,8 +301,9 @@ def tile_picked_wpna_none_l_kernel(
         pair[0] = pair_extremes(two, 0)
         extreme(0, 0)
         extreme(0, 1)
-        mean_in(0, True)
-        extremes_in(0, False)
+        two = pair_of(1)
+        extremes_in(0, True)
+        mean_in(0, False)
 
         third[1] = rounded(nc.scalar.copy, HALF, T - P)
         turn(HALF, 2, 8192)
@@ -310,7 +313,6 @@ def tile_picked_wpna_none_l_kernel(
         means[1] = mean_out(HALF, T - P)
         means[2] = mean_out(T - P, T)
 
-        two = pair_of(1)
         pair[1] = pair_extremes(two, 1)
         extreme(1, 0)
         extreme(1, 1)
@@ -319,6 +321,7 @@ def tile_picked_wpna_none_l_kernel(
         extreme(2, 1)
         mean_in(1, False)
         leave(1)
-        mean_in(2, True)
-        extremes_in(2, False)
+        for s in (largest, mean, smallest):
+            quantise(s, s + 1, T - P, means[2][:] if s == mean else flat(z[2][:, s - largest]))
+            products(accs[2], s, T - P, s == largest, s == smallest)
         leave(2)

@@ -69,14 +69,12 @@ def tile_picked_wpna_none_l_kernel(
                 out=xs[32 * q : 32 * q + 4, :].bitcast(I32), in_=x_scales[0, 4 * q : 4 * q + 4, :].bitcast(I32)
             )
         lists = [sb.tile([P, T // 16], U16, name="pos%d" % d) for d in range(3)]
-        for tile, pos in zip(lists[:2], (pos1, pos2)):
-            nc.sync.dma_start(tile[:], pos)
+        nc.sync.dma_start(lists[0][:], pos1)
         wz_raw = [sb.tile([P, PACK, N], F32, name="wz_raw%d" % s) for s in range(3)]
         for raw, w in zip(wz_raw, (w2, w3, w4)):
-            rows = w.rearrange("(g u r e) c -> u g r (e c)", u=2, r=RUN, e=2)
-            for u in range(2):
-                nc.sync.dma_start(out=raw[:, 2 * u : 2 * u + 2, :].rearrange("p e c -> p (e c)"), in_=rows[u])
+            nc.sync.dma_start(out=raw[:], in_=w.rearrange("(p t) c -> p t c", t=PACK))
             if raw is wz_raw[0]:
+                nc.sync.dma_start(lists[1][:], pos2)
                 nc.sync.dma_start(lists[2][:], pos3)
 
 
@@ -87,16 +85,13 @@ def tile_picked_wpna_none_l_kernel(
         h = [h_all[:, (PACK - 1 - t) * T : (PACK - t) * T] for t in range(PACK)]
         wide = [h_all[:, (PACK - 1 - t) * T : (PACK + 1 - t) * T] for t in range(1, PACK)]
         w1_grp = shared.tile([P, PACK, P, PACK], BF16, name="w1_grp", align_bytes=64, offset=16384)
-        w1_from = [
-            raw[:].rearrange("p j (g u a i e) -> p u e g a j i", u=2, a=RUN // LINE, i=LINE, e=2) for raw in w1_raw
-        ]
-        w1_into = w1_grp[:].rearrange("p t (g a i) (s j) -> p s t g a j i", a=RUN // LINE, i=LINE, s=2)
+        w1_from = [raw[:].rearrange("p j (m u e) -> p u m j e", u=2, e=2) for raw in w1_raw]
+        w1_into = w1_grp[:].rearrange("p (u e) m (s j) -> p s u m j e", e=2, s=2)
         w1_codes = sb.tile([P, PACK, P], U32, name="w1_codes", align_bytes=64)
         w1_scales = sb.tile([P, PACK, P], U8, name="w1_scales", align_bytes=64)
-        groups = P // RUN
 
-        def w1_round(copy, s, t, g0=0, g1=groups):
-            copy(out=w1_into[:, s, t, g0:g1], in_=w1_from[s][:, t // 2, t % 2, g0:g1])
+        def w1_round(copy, s, u, m0=0, m1=P):
+            copy(out=w1_into[:, s, u, m0:m1], in_=w1_from[s][:, u, m0:m1])
 
         def w1_quantise(t, m0, m1):
             nc.vector.quantize_mx(
@@ -105,14 +100,11 @@ def tile_picked_wpna_none_l_kernel(
                 in_=w1_grp[:, t, m0:m1].rearrange("p m j -> p (m j)"),
             )
 
-        for a in range(RUN // LINE):
-            nc.scalar.activation(w1_into[:, 0, 3, :, a], w1_from[0][:, 1, 1, :, a], COPY)
-        for t in range(3):
-            w1_round(nc.vector.tensor_copy, 0, t)
-        w1_round(nc.vector.tensor_copy, 1, 0, 0, groups // 2)
-        w1_round(nc.vector.tensor_copy, 1, 0, groups // 2, groups)
-        w1_round(nc.scalar.copy, 1, 2)
-        w1_round(nc.scalar.copy, 1, 3)
+        nc.scalar.activation(w1_into[:, 0, 1], w1_from[0][:, 1], COPY)
+        w1_round(nc.vector.tensor_copy, 0, 0)
+        w1_round(nc.vector.tensor_copy, 1, 0, 0, P // 2)
+        w1_round(nc.vector.tensor_copy, 1, 0, P // 2, P)
+        w1_round(nc.scalar.copy, 1, 1)
         w1_quantise(0, 0, P // 2)
         w1_quantise(0, P // 2, P)
 
@@ -132,7 +124,6 @@ def tile_picked_wpna_none_l_kernel(
         project(0, 0, HALF, 7, nc.vector.tensor_copy)
         project(0, HALF, T - P, 0, nc.scalar.copy)
         project(0, T - P, T, 1, nc.scalar.copy)
-        w1_round(nc.vector.tensor_copy, 1, 1)
         for t, n_bank in ((1, 2), (2, 3), (3, 0)):
             w1_quantise(t, 0, P)
             project(t, 0, T, n_bank, nc.scalar.copy)
@@ -169,8 +160,8 @@ def tile_picked_wpna_none_l_kernel(
                 )
                 added[blk] = added[blk] + 1
 
-        for a in (0, HALF):
-            for d in range(2):
+        for d in range(2):
+            for a in (0, HALF):
                 gather(on_vector, d, 0, a, a + HALF)
         for d in range(2):
             gather(on_scalar, d, 2, 0, T)
@@ -186,9 +177,15 @@ def tile_picked_wpna_none_l_kernel(
         wz_grp = shared.tile([P, 3, N, PACK], BF16, name="wz_grp", align_bytes=64, offset=16384)
         wz_codes = sb.tile([P, 3, N], U32, name="wz_codes", align_bytes=64)
         wz_scales = sb.tile([P, 3, N], U8, name="wz_scales", align_bytes=64)
-        for s in range(2):
-            nc.gpsimd.tensor_scalar(wz_grp[:, s], wz_raw[s][:].rearrange("p t c -> p c t"), 1.0, 0.0, MULT, ADD)
-        interleave(nc.vector.tensor_copy, wz_grp[:, 2], wz_raw[2][:])
+        for s in range(3):
+            nc.gpsimd.tensor_scalar(
+                wz_grp[:, s],
+                wz_raw[s][:].rearrange("p t c -> p c t"),
+                1.0,
+                0.0,
+                MULT,
+                ADD,
+            )
         for s0, s1 in ((0, 2), (2, 3)):
             nc.vector.quantize_mx(
                 out=wz_codes[:, s0:s1].rearrange("p s c -> p (s c)").bitcast(FP8X4),
@@ -220,12 +217,13 @@ def tile_picked_wpna_none_l_kernel(
                 )
 
         def rounded(copy, a, b):
-            r = sb.tile([P, b - a, PACK], BF16, name="third%d" % a, align_bytes=64)
+            at = {0: 16448, HALF: 18496, T - P: 24704}[a]
+            r = shared.tile([P, b - a, PACK], BF16, name="third%d" % a, align_bytes=64, offset=at)
             interleave(copy, r[:], columns(2, a, b))
             return r
 
         def pair_of(half):
-            two = sb.tile([P, 2, HALF, PACK], BF16, name="two%d" % half, align_bytes=64)
+            two = shared.tile([P, 2, HALF, PACK], BF16, name="two%d" % half, align_bytes=64, offset=(12352, 20544)[half])
             interleave_many(two[:], lists12[:, :, :, half * HALF : (half + 1) * HALF])
             return two
 
@@ -305,14 +303,14 @@ def tile_picked_wpna_none_l_kernel(
         extremes_in(0, True)
         mean_in(0, False)
 
-        third[1] = rounded(nc.scalar.copy, HALF, T - P)
-        turn(HALF, 2, 8192)
         third[2] = rounded(nc.scalar.copy, T - P, T)
-        turn(T - P, 3, 5120)
+        turn(HALF, 2, 8192)
+        turn(T - P, 3, 9216)
         leave(0)
         means[1] = mean_out(HALF, T - P)
         means[2] = mean_out(T - P, T)
 
+        third[1] = rounded(nc.vector.tensor_copy, HALF, T - P)
         pair[1] = pair_extremes(two, 1)
         extreme(1, 0)
         extreme(1, 1)

@@ -17,8 +17,6 @@ FP4X4 = mybir.dt.float4_e2m1fn_x4
 COPY = mybir.ActivationFunctionType.Copy
 MAX = mybir.AluOpType.max
 MIN = mybir.AluOpType.min
-MULT = mybir.AluOpType.mult
-ADD = mybir.AluOpType.add
 
 P = 128
 PACK = 4
@@ -178,14 +176,7 @@ def tile_picked_wpna_none_l_kernel(
         wz_codes = sb.tile([P, 3, N], U32, name="wz_codes", align_bytes=64)
         wz_scales = sb.tile([P, 3, N], U8, name="wz_scales", align_bytes=64)
         for s in range(3):
-            nc.gpsimd.tensor_scalar(
-                wz_grp[:, s],
-                wz_raw[s][:].rearrange("p t c -> p c t"),
-                1.0,
-                0.0,
-                MULT,
-                ADD,
-            )
+            nc.gpsimd.tensor_copy(wz_grp[:, s], wz_raw[s][:].rearrange("p t c -> p c t"))
         for s0, s1 in ((0, 2), (2, 3)):
             nc.vector.quantize_mx(
                 out=wz_codes[:, s0:s1].rearrange("p s c -> p (s c)").bitcast(FP8X4),

@@ -83,13 +83,13 @@ def tile_picked_wpna_none_l_kernel(
         h = [h_all[:, (PACK - 1 - t) * T : (PACK - t) * T] for t in range(PACK)]
         wide = [h_all[:, (PACK - 1 - t) * T : (PACK + 1 - t) * T] for t in range(1, PACK)]
         w1_grp = shared.tile([P, PACK, P, PACK], BF16, name="w1_grp", align_bytes=64, offset=16384)
-        w1_from = [raw[:].rearrange("p j (m u e) -> p u m j e", u=2, e=2) for raw in w1_raw]
-        w1_into = w1_grp[:].rearrange("p (u e) m (s j) -> p s u m j e", e=2, s=2)
+        w1_from = [raw[:].rearrange("p j (m t) -> p t m j", t=PACK) for raw in w1_raw]
+        w1_into = w1_grp[:].rearrange("p t m (s j) -> p s t m j", s=2)
         w1_codes = sb.tile([P, PACK, P], U32, name="w1_codes", align_bytes=64)
         w1_scales = sb.tile([P, PACK, P], U8, name="w1_scales", align_bytes=64)
 
-        def w1_round(copy, s, u, m0=0, m1=P):
-            copy(out=w1_into[:, s, u, m0:m1], in_=w1_from[s][:, u, m0:m1])
+        def w1_round(copy, s, t, m0=0, m1=P):
+            copy(out=w1_into[:, s, t, m0:m1], in_=w1_from[s][:, t, m0:m1])
 
         def w1_quantise(t, m0, m1):
             nc.vector.quantize_mx(
@@ -98,11 +98,13 @@ def tile_picked_wpna_none_l_kernel(
                 in_=w1_grp[:, t, m0:m1].rearrange("p m j -> p (m j)"),
             )
 
-        nc.scalar.activation(w1_into[:, 0, 1], w1_from[0][:, 1], COPY)
-        w1_round(nc.vector.tensor_copy, 0, 0)
+        nc.scalar.activation(w1_into[:, 0, 3], w1_from[0][:, 3], COPY)
+        for t in range(3):
+            w1_round(nc.vector.tensor_copy, 0, t)
         w1_round(nc.vector.tensor_copy, 1, 0, 0, P // 2)
         w1_round(nc.vector.tensor_copy, 1, 0, P // 2, P)
-        w1_round(nc.scalar.copy, 1, 1)
+        w1_round(nc.scalar.copy, 1, 2)
+        w1_round(nc.scalar.copy, 1, 3)
         w1_quantise(0, 0, P // 2)
         w1_quantise(0, P // 2, P)
 
@@ -122,6 +124,7 @@ def tile_picked_wpna_none_l_kernel(
         project(0, 0, HALF, 7, nc.vector.tensor_copy)
         project(0, HALF, T - P, 0, nc.scalar.copy)
         project(0, T - P, T, 1, nc.scalar.copy)
+        w1_round(nc.vector.tensor_copy, 1, 1)
         for t, n_bank in ((1, 2), (2, 3), (3, 0)):
             w1_quantise(t, 0, P)
             project(t, 0, T, n_bank, nc.scalar.copy)

@@ -21,8 +21,8 @@ MIN = mybir.AluOpType.min
 P = 128
 PACK = 4
 LINE = 4
-RUN = 8
 HALF = T // 2
+LAST = T - P
 
 
 def tile_picked_wpna_none_l_kernel(
@@ -37,22 +37,14 @@ def tile_picked_wpna_none_l_kernel(
         def bank(n_bank, shape, name):
             return ps.tile(shape, F32, name=name, tag="bank%d" % n_bank)
 
-        def lines(planes):
-            return planes.rearrange("p t (c i) -> p c t i", i=LINE)
-
-        def woven(words):
-            return words.rearrange("p (c i) t -> p c t i", i=LINE)
+        def placed(name, shape, dtype, at):
+            return shared.tile(shape, dtype, name=name, align_bytes=64, offset=at)
 
         def flat(words):
             return words.rearrange("p v t -> p (v t)")
 
         def interleave(copy, dst, src):
-            copy(out=woven(dst), in_=lines(src))
-
-        def interleave_many(dst, src):
-            nc.vector.tensor_copy(
-                out=dst.rearrange("p s (c i) t -> p s c t i", i=LINE), in_=src.rearrange("p s t (c i) -> p s c t i", i=LINE)
-            )
+            copy(out=dst.rearrange("p (c i) t -> p c t i", i=LINE), in_=src.rearrange("p t (c i) -> p c t i", i=LINE))
 
         w1_rows = w1.rearrange("(p s j) c -> s p j c", s=2, j=2)
         w1_raw = [sb.tile([P, 2, H], F32, name="w1_raw%d" % s) for s in range(2)]
@@ -67,14 +59,12 @@ def tile_picked_wpna_none_l_kernel(
                 out=xs[32 * q : 32 * q + 4, :].bitcast(I32), in_=x_scales[0, 4 * q : 4 * q + 4, :].bitcast(I32)
             )
         lists = [sb.tile([P, T // 16], U16, name="pos%d" % d) for d in range(3)]
-        nc.sync.dma_start(lists[0][:], pos1)
-        wz_raw = [sb.tile([P, PACK, N], F32, name="wz_raw%d" % s) for s in range(3)]
+        wz_raw = [placed("wz_raw%d" % s, [P, PACK, N], F32, 32768 + 8192 * s) for s in range(3)]
         for raw, w in zip(wz_raw, (w2, w3, w4)):
             nc.sync.dma_start(out=raw[:], in_=w.rearrange("(p t) c -> p t c", t=PACK))
             if raw is wz_raw[0]:
-                nc.sync.dma_start(lists[1][:], pos2)
-                nc.sync.dma_start(lists[2][:], pos3)
-
+                for tile, pos in zip(lists, (pos1, pos2, pos3)):
+                    nc.sync.dma_start(tile[:], pos)
 
         ident = sb.tile([P, P], F32, name="ident")
         make_identity(nc, ident[:])
@@ -82,10 +72,10 @@ def tile_picked_wpna_none_l_kernel(
         h_all = sb.tile([P, PACK * T], F32, name="h_all")
         h = [h_all[:, (PACK - 1 - t) * T : (PACK - t) * T] for t in range(PACK)]
         wide = [h_all[:, (PACK - 1 - t) * T : (PACK + 1 - t) * T] for t in range(1, PACK)]
-        w1_grp = shared.tile([P, PACK, P, PACK], BF16, name="w1_grp", align_bytes=64, offset=16384)
+        w1_grp = placed("w1_grp", [P, PACK, P, PACK], BF16, 16384)
         w1_from = [raw[:].rearrange("p j (m t) -> p t m j", t=PACK) for raw in w1_raw]
         w1_into = w1_grp[:].rearrange("p t m (s j) -> p s t m j", s=2)
-        w1_codes = sb.tile([P, PACK, P], U32, name="w1_codes", align_bytes=64)
+        w1_codes = placed("w1_codes", [P, PACK, P], U32, 24576)
         w1_scales = sb.tile([P, PACK, P], U8, name="w1_scales", align_bytes=64)
 
         def w1_round(copy, s, t, m0=0, m1=P):
@@ -122,38 +112,33 @@ def tile_picked_wpna_none_l_kernel(
             copy(out=h[t][:, a:b], in_=acc[:])
 
         project(0, 0, HALF, 7, nc.vector.tensor_copy)
-        project(0, HALF, T - P, 0, nc.scalar.copy)
-        project(0, T - P, T, 1, nc.scalar.copy)
+        project(0, HALF, LAST, 0, nc.scalar.copy)
+        project(0, LAST, T, 1, nc.scalar.copy)
         w1_round(nc.vector.tensor_copy, 1, 1)
         for t, n_bank in ((1, 2), (2, 3), (3, 0)):
             w1_quantise(t, 0, P)
             project(t, 0, T, n_bank, nc.scalar.copy)
 
-        lists12 = sb.tile([P, 2, PACK, T], F32, name="lists12")
-        pieces = ((0, HALF), (HALF, T - P), (T - P, T))
-        list3 = [sb.tile([P, PACK, HALF], F32, name="list3_first")]
+        wz_grp = placed("wz_grp", [P, 3, N, PACK], BF16, 16384)
+        for s in range(3):
+            nc.gpsimd.tensor_copy(wz_grp[:, s], wz_raw[s][:].rearrange("p t c -> p c t"))
 
-        def on_vector(dst, src):
-            nc.vector.tensor_copy(dst, src)
-
-        def on_scalar(dst, src):
-            nc.scalar.activation(dst, src, COPY)
-
-        def columns(d, a, b):
-            if d == 2:
-                return list3[a // HALF][:, :, a % HALF : a % HALF + b - a]
-            return lists12[:, d, :, a:b]
-
+        fetched = [placed("fetched0", [P, PACK, T], F32, 4096)]
+        fetched.append(sb.tile([P, PACK, T], F32, name="fetched1"))
+        fetched.append(placed("fetched2", [P, PACK, T], F32, 32768))
         sums = [bank(4 + blk, [P, PACK, P], "sum%d" % blk) for blk in range(T // P)]
         added = [0] * len(sums)
 
-        def gather(fetch, d, t, a, b):
-            window = wide[t - 1] if b - a == T else h[t]
-            fetch(columns(d, a, b)[:, t], window.indirect(lists[d][:, a // 16 : b // 16]))
+        def gather(d, t, a, b):
+            window = (wide[t - 1] if b - a == T else h[t]).indirect(lists[d][:, a // 16 : b // 16])
+            if t < 2:
+                nc.vector.tensor_copy(fetched[d][:, t, a:b], window)
+            else:
+                nc.scalar.activation(fetched[d][:, t, a:b], window, COPY)
             for blk in range(a // P, b // P):
                 nc.tensor.matmul(
                     sums[blk][:, t, :],
-                    lhsT=columns(d, blk * P, (blk + 1) * P)[:, t],
+                    lhsT=fetched[d][:, t, blk * P : (blk + 1) * P],
                     rhs=ident[:],
                     is_transpose=True,
                     start=added[blk] == 0,
@@ -161,114 +146,117 @@ def tile_picked_wpna_none_l_kernel(
                 )
                 added[blk] = added[blk] + 1
 
-        for d in range(2):
-            for a in (0, HALF):
-                gather(on_vector, d, 0, a, a + HALF)
-        for d in range(2):
-            gather(on_scalar, d, 2, 0, T)
-            gather(on_vector, d, 1, 0, T)
-        gather(on_scalar, 0, 3, 0, T)
-        for t in range(2):
-            gather(on_vector, 2, t, 0, HALF)
-        gather(on_scalar, 1, 3, 0, HALF)
-        for t in range(2, PACK):
-            gather(on_scalar, 2, t, 0, HALF)
-        gather(on_scalar, 1, 3, HALF, T)
+        gather(0, 0, 0, HALF)
+        gather(0, 0, HALF, T)
+        gather(1, 0, 0, HALF)
+        gather(0, 2, 0, HALF)
+        gather(0, 3, 0, HALF)
+        gather(0, 1, 0, T)
+        gather(0, 2, HALF, T)
+        gather(1, 0, HALF, T)
+        gather(0, 3, HALF, T)
+        gather(1, 1, 0, T)
+        gather(1, 2, 0, T)
+        gather(2, 0, 0, HALF)
+        gather(2, 1, 0, T)
+        gather(1, 3, 0, HALF)
+        gather(2, 0, HALF, T)
+        gather(2, 2, 0, HALF)
+        gather(2, 3, 0, HALF)
+        gather(1, 3, HALF, T)
+        gather(2, 2, HALF, T)
+        gather(2, 3, HALF, T)
 
-        wz_grp = shared.tile([P, 3, N, PACK], BF16, name="wz_grp", align_bytes=64, offset=16384)
-        wz_codes = sb.tile([P, 3, N], U32, name="wz_codes", align_bytes=64)
+        first = [placed("first%d" % half, [P, HALF, PACK], BF16, 49152 + 2048 * half) for half in range(2)]
+        for half in range(2):
+            nc.gpsimd.tensor_copy(
+                first[half][:], fetched[0][:, :, half * HALF : (half + 1) * HALF].rearrange("p t v -> p v t")
+            )
+
+        wz_codes = placed("wz_codes", [P, 3, N], U32, 1088)
         wz_scales = sb.tile([P, 3, N], U8, name="wz_scales", align_bytes=64)
-        for s in range(3):
-            nc.gpsimd.tensor_copy(wz_grp[:, s], wz_raw[s][:].rearrange("p t c -> p c t"))
-        for s0, s1 in ((0, 2), (2, 3)):
+
+        def wz_quantise(s0, s1):
             nc.vector.quantize_mx(
                 out=wz_codes[:, s0:s1].rearrange("p s c -> p (s c)").bitcast(FP8X4),
                 scales=wz_scales[:, s0:s1].rearrange("p s c -> p (s c)"),
                 in_=wz_grp[:, s0:s1].rearrange("p s c j -> p (s c j)"),
             )
 
-        z_codes = {a: sb.tile([P, 3, b - a], U32, name="z_codes%d" % a, align_bytes=64) for a, b in pieces}
-        z_scales = {a: sb.tile([P, 3, b - a], U8, name="z_scales%d" % a, align_bytes=64) for a, b in pieces}
+        pieces = ((0, HALF), (HALF, LAST), (LAST, T))
+        z_codes = [placed("z_codes0", [P, 3, HALF], U32, 16384)]
+        z_codes.extend(sb.tile([P, 3, P], U32, name="z_codes%d" % n, align_bytes=64) for n in (1, 2))
+        z_scales = [sb.tile([P, 3, b - a], U8, name="z_scales%d" % a, align_bytes=64) for a, b in pieces]
         mean, largest, smallest = range(3)
 
-        def quantise(s0, s1, a, z):
+        def quantise(n, s0, s1, values):
             nc.vector.quantize_mx(
-                out=z_codes[a][:, s0:s1].rearrange("p s v -> p (s v)").bitcast(FP8X4),
-                scales=z_scales[a][:, s0:s1].rearrange("p s v -> p (s v)"),
-                in_=z,
+                out=z_codes[n][:, s0:s1].rearrange("p s v -> p (s v)").bitcast(FP8X4),
+                scales=z_scales[n][:, s0:s1].rearrange("p s v -> p (s v)"),
+                in_=values,
             )
 
-        def products(accs, s, a, start, stop):
+        def products(n, s, start, stop):
+            apart = n == 2
             for mt in range(2):
                 nc.tensor.matmul_mx(
-                    out=accs[mt],
+                    out=accs[n][mt],
                     lhsT=wz_codes[:, s, mt * P : (mt + 1) * P].bitcast(FP8X4),
                     lhsT_scale=wz_scales[:, s, mt * P : (mt + 1) * P],
-                    rhs=z_codes[a][:, s].bitcast(FP8X4),
-                    rhs_scale=z_scales[a][:, s],
-                    start=start and (mt == 0 or a == T - P),
-                    stop=stop and (mt == 1 or a == T - P),
+                    rhs=z_codes[n][:, s].bitcast(FP8X4),
+                    rhs_scale=z_scales[n][:, s],
+                    start=start and (mt == 0 or apart),
+                    stop=stop and (mt == 1 or apart),
                 )
 
-        def rounded(copy, a, b):
-            at = {0: 16448, HALF: 18496, T - P: 24704}[a]
-            r = shared.tile([P, b - a, PACK], BF16, name="third%d" % a, align_bytes=64, offset=at)
-            interleave(copy, r[:], columns(2, a, b))
+        def rounded(copy, d, a, b, r):
+            interleave(copy, r[:], fetched[d][:, :, a:b])
             return r
 
-        def pair_of(half):
-            two = shared.tile([P, 2, HALF, PACK], BF16, name="two%d" % half, align_bytes=64, offset=(12352, 20544)[half])
-            interleave_many(two[:], lists12[:, :, :, half * HALF : (half + 1) * HALF])
-            return two
+        def pair_extreme(half, side):
+            nc.vector.tensor_tensor(flat(pair[half][:, side]), flat(first[half][:]), flat(second[half][:]), (MAX, MIN)[side])
 
-        def pair_extremes(two, half):
-            pair = sb.tile([P, 2, HALF, PACK], BF16, name="pair%d" % half, align_bytes=64)
-            for side, op in enumerate((MAX, MIN)):
-                nc.vector.tensor_tensor(flat(pair[:, side]), flat(two[:, 0]), flat(two[:, 1]), op)
-            return pair
+        words = [bank(n, [P, (b - a) // P, 2, P], "words%d" % a) for n, (a, b) in enumerate(pieces)]
 
-        words = {a: bank(n, [P, (b - a) // P, 2, P], "words%d" % a) for n, (a, b) in enumerate(pieces)}
-
-        def turn(a, blk, at):
-            staged = shared.tile([P, 2, P, 2], BF16, name="staged%d" % blk, offset=at)
+        def turn(n, blk, staged):
             nc.scalar.activation(
                 staged[:], sums[blk][:].rearrange("v (u e) p -> v u p e", e=2), COPY, scale=1.0 / 3.0
             )
             pairs = staged[:].rearrange("v u p e -> v (u p e)").bitcast(F32)
             for u in range(2):
-                nc.tensor.transpose(words[a][:, blk - a // P, u, :], pairs[:, u * P : (u + 1) * P], ident[:])
+                nc.tensor.transpose(words[n][:, blk - pieces[n][0] // P, u, :], pairs[:, u * P : (u + 1) * P], ident[:])
 
-        def mean_out(a, b):
+        def mean_out(n):
+            a, b = pieces[n]
             z_mean = sb.tile([P, (b - a) * PACK], BF16, name="z_mean%d" % a, align_bytes=64)
             nc.scalar.copy(
                 out=z_mean[:].bitcast(F32).rearrange("p (b v u) -> p b v u", v=P, u=2),
-                in_=words[a][:].rearrange("p b u v -> p b v u"),
+                in_=words[n][:].rearrange("p b u v -> p b v u"),
             )
             return z_mean
 
         out_rows = out.rearrange("(mt p) v -> p mt v", p=P)
-        z = [shared.tile([P, 2, HALF, PACK], BF16, name="z_first", align_bytes=64, offset=8192)]
-        z.extend(sb.tile([P, 2, P, PACK], BF16, name="z%d" % a, align_bytes=64) for a, b in pieces[1:])
+        z = [placed("z_first", [P, 2, HALF, PACK], BF16, 28672)]
+        z.extend(sb.tile([P, 2, P, PACK], BF16, name="z%d" % n, align_bytes=64) for n in (1, 2))
         joint = [bank(3, [P, 2, HALF], "o_first"), bank(4, [P, 2, P], "o_middle")]
         accs = [[acc[:, mt] for mt in range(2)] for acc in joint]
         accs.append([bank(5 * mt, [P, P], "o_last%d" % mt)[:] for mt in range(2)])
-        pair, third, means = {}, {}, {}
+        pair = [sb.tile([P, 2, HALF, PACK], BF16, name="pair%d" % half, align_bytes=64) for half in range(2)]
+        second, third, means = {}, {}, {}
 
         def extreme(n, side):
             a, b = pieces[n]
             two = pair[a // HALF][:, side, a % HALF : a % HALF + b - a]
             nc.vector.tensor_tensor(flat(z[n][:, side]), flat(two), flat(third[n][:]), (MAX, MIN)[side])
 
-        def extremes_in(n, start):
-            a = pieces[n][0]
-            quantise(largest, 3, a, z[n][:].rearrange("p s v t -> p (s v t)"))
-            products(accs[n], largest, a, start, False)
-            products(accs[n], smallest, a, False, not start)
+        def extremes_in(n):
+            quantise(n, largest, 3, z[n][:].rearrange("p s v t -> p (s v t)"))
+            products(n, largest, True, False)
+            products(n, smallest, False, False)
 
-        def mean_in(n, start):
-            a = pieces[n][0]
-            quantise(mean, largest, a, means[n][:])
-            products(accs[n], mean, a, start, not start)
+        def mean_in(n):
+            quantise(n, mean, largest, means[n][:])
+            products(n, mean, False, True)
 
         def leave(n):
             a, b = pieces[n]
@@ -281,39 +269,41 @@ def tile_picked_wpna_none_l_kernel(
                 nc.scalar.copy(out=res[:], in_=joint[n][:])
                 nc.sync.dma_start(out=out_rows[:, :, a:b], in_=res[:])
 
-        turn(0, 0, 0)
-        turn(0, 1, 4096)
-        means[0] = mean_out(0, HALF)
-        list3.append(shared.tile([P, PACK, HALF], F32, name="list3_last", offset=0))
-        for t in range(PACK):
-            gather(on_scalar, 2, t, HALF, T)
+        for blk in range(2):
+            turn(0, blk, sb.tile([P, 2, P, 2], BF16, name="staged%d" % blk))
+        for n in (1, 2):
+            a, b = pieces[n]
+            third[n] = rounded(nc.scalar.copy, 2, a, b, sb.tile([P, P, PACK], BF16, name="third%d" % n, align_bytes=64))
+        means[0] = mean_out(0)
 
-        two = pair_of(0)
-        third[0] = rounded(nc.vector.tensor_copy, 0, HALF)
-        pair[0] = pair_extremes(two, 0)
+        wz_quantise(0, 2)
+        second[0] = rounded(nc.vector.tensor_copy, 1, 0, HALF, placed("second0", [P, HALF, PACK], BF16, 4160))
+        wz_quantise(2, 3)
+        third[0] = rounded(nc.vector.tensor_copy, 2, 0, HALF, placed("third0", [P, HALF, PACK], BF16, 6208))
+        pair_extreme(0, 0)
+        pair_extreme(0, 1)
         extreme(0, 0)
         extreme(0, 1)
-        two = pair_of(1)
-        extremes_in(0, True)
-        mean_in(0, False)
+        second[1] = rounded(nc.vector.tensor_copy, 1, HALF, T, placed("second1", [P, HALF, PACK], BF16, 8256))
+        extremes_in(0)
 
-        third[2] = rounded(nc.scalar.copy, T - P, T)
-        turn(HALF, 2, 8192)
-        turn(T - P, 3, 9216)
+        turn(1, 2, placed("staged2", [P, 2, P, 2], BF16, 28672))
+        turn(2, 3, placed("staged3", [P, 2, P, 2], BF16, 29696))
+        means[1] = mean_out(1)
+        means[2] = mean_out(2)
+
+        pair_extreme(1, 0)
+        pair_extreme(1, 1)
+        mean_in(0)
         leave(0)
-        means[1] = mean_out(HALF, T - P)
-        means[2] = mean_out(T - P, T)
-
-        third[1] = rounded(nc.vector.tensor_copy, HALF, T - P)
-        pair[1] = pair_extremes(two, 1)
         extreme(1, 0)
         extreme(1, 1)
         extreme(2, 0)
-        extremes_in(1, True)
+        extremes_in(1)
         extreme(2, 1)
-        mean_in(1, False)
+        mean_in(1)
         leave(1)
         for s in (largest, mean, smallest):
-            quantise(s, s + 1, T - P, means[2][:] if s == mean else flat(z[2][:, s - largest]))
-            products(accs[2], s, T - P, s == largest, s == smallest)
+            quantise(2, s, s + 1, means[2][:] if s == mean else flat(z[2][:, s - largest]))
+            products(2, s, s == largest, s == smallest)
         leave(2)

@@ -121,7 +121,7 @@ def tile_picked_wpna_none_l_kernel(
 
         wz_grp = placed("wz_grp", [P, 3, N, PACK], BF16, 16384)
         for s in range(3):
-            nc.gpsimd.tensor_copy(wz_grp[:, s], wz_raw[s][:].rearrange("p t c -> p c t"))
+            interleave(nc.gpsimd.tensor_copy, wz_grp[:, s], wz_raw[s][:])
 
         fetched = [placed("fetched0", [P, PACK, T], F32, 4096)]
         fetched.append(sb.tile([P, PACK, T], F32, name="fetched1"))
@@ -169,9 +169,7 @@ def tile_picked_wpna_none_l_kernel(
 
         first = [placed("first%d" % half, [P, HALF, PACK], BF16, 49152 + 2048 * half) for half in range(2)]
         for half in range(2):
-            nc.gpsimd.tensor_copy(
-                first[half][:], fetched[0][:, :, half * HALF : (half + 1) * HALF].rearrange("p t v -> p v t")
-            )
+            interleave(nc.gpsimd.tensor_copy, first[half][:], fetched[0][:, :, half * HALF : (half + 1) * HALF])
 
         wz_codes = placed("wz_codes", [P, 3, N], U32, 1088)
         wz_scales = sb.tile([P, 3, N], U8, name="wz_scales", align_bytes=64)

from contextlib import ExitStack

import concourse.mybir as mybir
from concourse.masks import make_identity

K, T, H, N = 512, 512, 512, 256
FLOPS = 2 * K * H * T + 3 * 2 * H * N * T

F32 = mybir.dt.float32
BF16 = mybir.dt.bfloat16
I32 = mybir.dt.int32
U32 = mybir.dt.uint32
U16 = mybir.dt.uint16
U8 = mybir.dt.uint8
FP8X4 = mybir.dt.float8_e4m3fn_x4
FP4X4 = mybir.dt.float4_e2m1fn_x4
COPY = mybir.ActivationFunctionType.Copy
MAX = mybir.AluOpType.max
MIN = mybir.AluOpType.min

P = 128
PACK = 4
LINE = 4
HALF = T // 2
LAST = T - P


def tile_picked_wpna_none_l_kernel(
    tc, x_words, x_scales, w1, w2, w3, w4, pos1, pos2, pos3, out
):
    nc = tc.nc
    with ExitStack() as ctx:
        sb = ctx.enter_context(tc.tile_pool(name="sb", bufs=1))
        shared = ctx.enter_context(tc.tile_pool(name="shared", bufs=1))
        ps = ctx.enter_context(tc.psum_pool(name="ps", bufs=1))

        def bank(n_bank, shape, name):
            return ps.tile(shape, F32, name=name, tag="bank%d" % n_bank)

        def placed(name, shape, dtype, at):
            return shared.tile(shape, dtype, name=name, align_bytes=64, offset=at)

        def flat(words):
            return words.rearrange("p v t -> p (v t)")

        def interleave(copy, dst, src):
            copy(out=dst.rearrange("p (c i) t -> p c t i", i=LINE), in_=src.rearrange("p t (c i) -> p c t i", i=LINE))

        w1_rows = w1.rearrange("(p s j) c -> s p j c", s=2, j=2)
        w1_raw = [sb.tile([P, 2, H], F32, name="w1_raw%d" % s) for s in range(2)]
        for s in range(2):
            nc.sync.dma_start(out=w1_raw[s][:], in_=w1_rows[s])
        xw = sb.tile([P, 2 * T], U8, name="xw", align_bytes=64)
        nc.sync.dma_start(out=xw[:].bitcast(I32), in_=x_words[0].bitcast(I32))
        xs = sb.tile([P, T], U8, name="xs", align_bytes=64)
        nc.vector.memset(xs[:].bitcast(I32), 0)
        for q in range(4):
            nc.sync.dma_start(
                out=xs[32 * q : 32 * q + 4, :].bitcast(I32), in_=x_scales[0, 4 * q : 4 * q + 4, :].bitcast(I32)
            )
        lists = [sb.tile([P, T // 16], U16, name="pos%d" % d) for d in range(3)]
        wz_raw = [placed("wz_raw%d" % s, [P, PACK, N], F32, 32768 + 8192 * s) for s in range(3)]
        for raw, w in zip(wz_raw, (w2, w3, w4)):
            nc.sync.dma_start(out=raw[:], in_=w.rearrange("(p t) c -> p t c", t=PACK))
            if raw is wz_raw[0]:
                for tile, pos in zip(lists, (pos1, pos2, pos3)):
                    nc.sync.dma_start(tile[:], pos)

        ident = sb.tile([P, P], F32, name="ident")
        make_identity(nc, ident[:])

        h_all = sb.tile([P, PACK * T], F32, name="h_all")
        h = [h_all[:, (PACK - 1 - t) * T : (PACK - t) * T] for t in range(PACK)]
        wide = [h_all[:, (PACK - 1 - t) * T : (PACK + 1 - t) * T] for t in range(1, PACK)]
        w1_grp = placed("w1_grp", [P, PACK, P, PACK], BF16, 16384)
        w1_from = [raw[:].rearrange("p j (m t) -> p t m j", t=PACK) for raw in w1_raw]
        w1_into = w1_grp[:].rearrange("p t m (s j) -> p s t m j", s=2)
        w1_codes = placed("w1_codes", [P, PACK, P], U32, 24576)
        w1_scales = sb.tile([P, PACK, P], U8, name="w1_scales", align_bytes=64)

        def w1_round(copy, s, t, m0=0, m1=P):
            copy(out=w1_into[:, s, t, m0:m1], in_=w1_from[s][:, t, m0:m1])

        def w1_quantise(t, m0, m1):
            nc.vector.quantize_mx(
                out=w1_codes[:, t, m0:m1].bitcast(FP8X4),
                scales=w1_scales[:, t, m0:m1],
                in_=w1_grp[:, t, m0:m1].rearrange("p m j -> p (m j)"),
            )

        nc.scalar.activation(w1_into[:, 0, 3], w1_from[0][:, 3], COPY)
        for t in range(3):
            w1_round(nc.vector.tensor_copy, 0, t)
        w1_round(nc.vector.tensor_copy, 1, 0, 0, P // 2)
        w1_round(nc.vector.tensor_copy, 1, 0, P // 2, P)
        w1_round(nc.scalar.copy, 1, 2)
        w1_round(nc.scalar.copy, 1, 3)
        w1_quantise(0, 0, P // 2)
        w1_quantise(0, P // 2, P)

        def project(t, a, b, n_bank, copy):
            acc = bank(n_bank, [P, b - a], "h_acc%d_%d" % (t, a))
            nc.tensor.matmul_mx(
                out=acc[:],
                lhsT=w1_codes[:, t, :].bitcast(FP8X4),
                lhsT_scale=w1_scales[:, t, :],
                rhs=xw[:, 2 * a : 2 * b].bitcast(FP4X4),
                rhs_scale=xs[:, a:b],
                start=True,
                stop=True,
            )
            copy(out=h[t][:, a:b], in_=acc[:])

        project(0, 0, HALF, 7, nc.vector.tensor_copy)
        project(0, HALF, LAST, 0, nc.scalar.copy)
        project(0, LAST, T, 1, nc.scalar.copy)
        w1_round(nc.vector.tensor_copy, 1, 1)
        for t, n_bank in ((1, 2), (2, 3), (3, 0)):
            w1_quantise(t, 0, P)
            project(t, 0, T, n_bank, nc.scalar.copy)

        wz_grp = placed("wz_grp", [P, 3, N, PACK], BF16, 16384)
        for s in range(3):
            interleave(nc.gpsimd.tensor_copy, wz_grp[:, s], wz_raw[s][:])

        fetched = [placed("fetched0", [P, PACK, T], F32, 4096)]
        fetched.append(sb.tile([P, PACK, T], F32, name="fetched1"))
        fetched.append(placed("fetched2", [P, PACK, T], F32, 32768))
        sums = [bank(4 + blk, [P, PACK, P], "sum%d" % blk) for blk in range(T // P)]
        added = [0] * len(sums)

        def gather(d, t, a, b):
            window = (wide[t - 1] if b - a == T else h[t]).indirect(lists[d][:, a // 16 : b // 16])
            if t < 2:
                nc.vector.tensor_copy(fetched[d][:, t, a:b], window)
            else:
                nc.scalar.activation(fetched[d][:, t, a:b], window, COPY)
            for blk in range(a // P, b // P):
                nc.tensor.matmul(
                    sums[blk][:, t, :],
                    lhsT=fetched[d][:, t, blk * P : (blk + 1) * P],
                    rhs=ident[:],
                    is_transpose=True,
                    start=added[blk] == 0,
                    stop=added[blk] == 3 * PACK - 1,
                )
                added[blk] = added[blk] + 1

        gather(0, 0, 0, HALF)
        gather(0, 0, HALF, T)
        gather(1, 0, 0, HALF)
        gather(0, 2, 0, HALF)
        gather(0, 3, 0, HALF)
        gather(0, 1, 0, T)
        gather(0, 2, HALF, T)
        gather(1, 0, HALF, T)
        gather(0, 3, HALF, T)
        gather(1, 1, 0, T)
        gather(1, 2, 0, T)
        gather(2, 0, 0, HALF)
        gather(2, 1, 0, T)
        gather(1, 3, 0, HALF)
        gather(2, 0, HALF, T)
        gather(2, 2, 0, HALF)
        gather(2, 3, 0, HALF)
        gather(1, 3, HALF, T)
        gather(2, 2, HALF, T)
        gather(2, 3, HALF, T)

        first = [placed("first%d" % half, [P, HALF, PACK], BF16, 49152 + 2048 * half) for half in range(2)]
        for half in range(2):
            interleave(nc.gpsimd.tensor_copy, first[half][:], fetched[0][:, :, half * HALF : (half + 1) * HALF])

        wz_codes = placed("wz_codes", [P, 3, N], U32, 1088)
        wz_scales = sb.tile([P, 3, N], U8, name="wz_scales", align_bytes=64)

        def wz_quantise(s0, s1):
            nc.vector.quantize_mx(
                out=wz_codes[:, s0:s1].rearrange("p s c -> p (s c)").bitcast(FP8X4),
                scales=wz_scales[:, s0:s1].rearrange("p s c -> p (s c)"),
                in_=wz_grp[:, s0:s1].rearrange("p s c j -> p (s c j)"),
            )

        pieces = ((0, HALF), (HALF, LAST), (LAST, T))
        z_codes = [placed("z_codes0", [P, 3, HALF], U32, 16384)]
        z_codes.extend(sb.tile([P, 3, P], U32, name="z_codes%d" % n, align_bytes=64) for n in (1, 2))
        z_scales = [sb.tile([P, 3, b - a], U8, name="z_scales%d" % a, align_bytes=64) for a, b in pieces]
        mean, largest, smallest = range(3)

        def quantise(n, s0, s1, values):
            nc.vector.quantize_mx(
                out=z_codes[n][:, s0:s1].rearrange("p s v -> p (s v)").bitcast(FP8X4),
                scales=z_scales[n][:, s0:s1].rearrange("p s v -> p (s v)"),
                in_=values,
            )

        def products(n, s, start, stop):
            apart = n == 2
            for mt in range(2):
                nc.tensor.matmul_mx(
                    out=accs[n][mt],
                    lhsT=wz_codes[:, s, mt * P : (mt + 1) * P].bitcast(FP8X4),
                    lhsT_scale=wz_scales[:, s, mt * P : (mt + 1) * P],
                    rhs=z_codes[n][:, s].bitcast(FP8X4),
                    rhs_scale=z_scales[n][:, s],
                    start=start and (mt == 0 or apart),
                    stop=stop and (mt == 1 or apart),
                )

        def rounded(copy, d, a, b, r):
            interleave(copy, r[:], fetched[d][:, :, a:b])
            return r

        def pair_extreme(half, side):
            nc.vector.tensor_tensor(flat(pair[half][:, side]), flat(first[half][:]), flat(second[half][:]), (MAX, MIN)[side])

        words = [bank(n, [P, (b - a) // P, 2, P], "words%d" % a) for n, (a, b) in enumerate(pieces)]

        def turn(n, blk, staged):
            nc.scalar.activation(
                staged[:], sums[blk][:].rearrange("v (u e) p -> v u p e", e=2), COPY, scale=1.0 / 3.0
            )
            pairs = staged[:].rearrange("v u p e -> v (u p e)").bitcast(F32)
            for u in range(2):
                nc.tensor.transpose(words[n][:, blk - pieces[n][0] // P, u, :], pairs[:, u * P : (u + 1) * P], ident[:])

        def mean_out(n):
            a, b = pieces[n]
            z_mean = sb.tile([P, (b - a) * PACK], BF16, name="z_mean%d" % a, align_bytes=64)
            nc.scalar.copy(
                out=z_mean[:].bitcast(F32).rearrange("p (b v u) -> p b v u", v=P, u=2),
                in_=words[n][:].rearrange("p b u v -> p b v u"),
            )
            return z_mean

        out_rows = out.rearrange("(mt p) v -> p mt v", p=P)
        z = [placed("z_first", [P, 2, HALF, PACK], BF16, 28672)]
        z.extend(sb.tile([P, 2, P, PACK], BF16, name="z%d" % n, align_bytes=64) for n in (1, 2))
        joint = [bank(3, [P, 2, HALF], "o_first"), bank(4, [P, 2, P], "o_middle")]
        accs = [[acc[:, mt] for mt in range(2)] for acc in joint]
        accs.append([bank(5 * mt, [P, P], "o_last%d" % mt)[:] for mt in range(2)])
        pair = [sb.tile([P, 2, HALF, PACK], BF16, name="pair%d" % half, align_bytes=64) for half in range(2)]
        second, third, means = {}, {}, {}

        def extreme(n, side):
            a, b = pieces[n]
            two = pair[a // HALF][:, side, a % HALF : a % HALF + b - a]
            nc.vector.tensor_tensor(flat(z[n][:, side]), flat(two), flat(third[n][:]), (MAX, MIN)[side])

        def extremes_in(n):
            quantise(n, largest, 3, z[n][:].rearrange("p s v t -> p (s v t)"))
            products(n, largest, True, False)
            products(n, smallest, False, False)

        def mean_in(n):
            quantise(n, mean, largest, means[n][:])
            products(n, mean, False, True)

        def leave(n):
            a, b = pieces[n]
            res = sb.tile([P, 2, b - a], F32, name="res%d" % a, align_bytes=64)
            if b == T:
                for mt in range(2):
                    (nc.scalar.copy, nc.vector.tensor_copy)[mt](out=res[:, mt, :], in_=accs[n][mt])
                    nc.sync.dma_start(out=out_rows[:, mt, a:b], in_=res[:, mt, :])
            else:
                nc.scalar.copy(out=res[:], in_=joint[n][:])
                nc.sync.dma_start(out=out_rows[:, :, a:b], in_=res[:])

        for blk in range(2):
            turn(0, blk, sb.tile([P, 2, P, 2], BF16, name="staged%d" % blk))
        for n in (1, 2):
            a, b = pieces[n]
            third[n] = rounded(nc.scalar.copy, 2, a, b, sb.tile([P, P, PACK], BF16, name="third%d" % n, align_bytes=64))
        means[0] = mean_out(0)

        wz_quantise(0, 2)
        second[0] = rounded(nc.vector.tensor_copy, 1, 0, HALF, placed("second0", [P, HALF, PACK], BF16, 4160))
        wz_quantise(2, 3)
        third[0] = rounded(nc.vector.tensor_copy, 2, 0, HALF, placed("third0", [P, HALF, PACK], BF16, 6208))
        pair_extreme(0, 0)
        pair_extreme(0, 1)
        extreme(0, 0)
        extreme(0, 1)
        second[1] = rounded(nc.vector.tensor_copy, 1, HALF, T, placed("second1", [P, HALF, PACK], BF16, 8256))
        extremes_in(0)

        turn(1, 2, placed("staged2", [P, 2, P, 2], BF16, 28672))
        turn(2, 3, placed("staged3", [P, 2, P, 2], BF16, 29696))
        means[1] = mean_out(1)
        means[2] = mean_out(2)

        pair_extreme(1, 0)
        pair_extreme(1, 1)
        mean_in(0)
        leave(0)
        extreme(1, 0)
        extreme(1, 1)
        extreme(2, 0)
        extremes_in(1)
        extreme(2, 1)
        mean_in(1)
        leave(1)
        for s in (largest, mean, smallest):
            quantise(2, s, s + 1, means[2][:] if s == mean else flat(z[2][:, s - largest]))
            products(2, s, s == largest, s == smallest)
        leave(2)
